import numpy as np
import ml_dtypes


def mxq(x, axis, fmt="e4m3"):
    dtype, down = {"e4m3": (ml_dtypes.float8_e4m3fn, 7), "e5m2": (ml_dtypes.float8_e5m2, 14)}[fmt]
    v = np.moveaxis(np.asarray(x, np.float32).astype(ml_dtypes.bfloat16).astype(np.float64), axis, -1)
    blocks = v.reshape(v.shape[:-1] + (-1, 32))
    amax = np.abs(blocks).max(-1, keepdims=True)
    byte = np.maximum(np.where(amax > 0, np.frexp(amax)[1] - 1 + 127, 0) - down, 1)
    scale = np.exp2(byte - 127.0)
    codes = (blocks / scale).astype(np.float32).astype(dtype).astype(np.float64)
    return np.moveaxis((codes * scale).reshape(v.shape), -1, axis)


WIDE = False


def mx_kscale(k):
    if not WIDE:
        return np.ones(k)
    levels = np.array([10, -10, 5, -5, 0])
    if k % 512:
        return np.exp2(np.random.permutation(np.resize(levels, k // 32))).repeat(32)
    a = np.empty((k // 512, 16))
    for p in range(k // 512):
        a[p, :8] = np.random.permutation(np.resize(levels, 8))
        for g in range(8):
            far = levels[np.abs(levels - a[p, g]) >= 10]
            a[p, g + 8] = far[np.random.randint(len(far))]
    return np.exp2(a.ravel()).repeat(32)


def f64(x):
    return np.asarray(x).astype(np.float64)


def striped(idx):
    return np.tile(idx.reshape(-1, 16).T, (8, 1)).astype(np.uint16)


def unstriped(offs):
    return offs[:16].T.reshape(-1).astype(np.int64)


def silu(v):
    return v / (1.0 + np.exp(-np.maximum(v, -700.0)))


K, T, S, V, H, N = 512, 1024, 512, 1024, 512, 256
P = 2 ** 7


def setup_inputs():
    n = np.random.standard_normal
    s = mx_kscale(K)[:, None]
    u = mx_kscale(H)
    return {
        "xT": (n((K, T)) * s).astype(np.float32),
        "w1": (n((K, H)) / np.sqrt(K) / s * u).astype(np.float32),
        "w2": (n((H, N)) / np.sqrt(H) / u[:, None]).astype(np.float32),
        "gate": np.tile(np.random.uniform(0.5, 1.5, S), (P, 1)).astype(np.float32),
        "offs": striped(np.random.permutation(T)[:S]),
        "pos1": striped(np.random.permutation(V)[:S]),
    }


def reference(xT, w1, w2, gate, offs, pos1):
    h = silu(mxq(f64(w1), 0, "e4m3").T @ mxq(f64(xT)[:, unstriped(offs)], 0, "e4m3"))
    z = np.zeros((H, V))
    z[:, unstriped(pos1)] = f64(gate)[:1] * h
    return mxq(f64(w2), 0, "e4m3").T @ mxq(z, 0, "e4m3")

@@ -1,0 +1,200 @@
+from contextlib import ExitStack
+
+import concourse.mybir as mybir
+
+K, T, S, V, H, N = 512, 1024, 512, 1024, 512, 256
+FLOPS = 2 * K * H * S + 2 * H * N * V
+
+F32 = mybir.dt.float32
+BF16 = mybir.dt.bfloat16
+U32 = mybir.dt.uint32
+U16 = mybir.dt.uint16
+U8 = mybir.dt.uint8
+FP8X4 = mybir.dt.float8_e4m3fn_x4
+SILU = mybir.ActivationFunctionType.Silu
+MULT = mybir.AluOpType.mult
+
+P = 128
+HALF = 256
+
+
+def tile_picked_voxel_silu_e_kernel(tc, xT, w1, w2, gate, offs, pos1, out):
+    nc = tc.nc
+    with ExitStack() as ctx:
+        held = ctx.enter_context(tc.tile_pool(name="held", bufs=1))
+        psum = ctx.enter_context(tc.psum_pool(name="psum", bufs=8))
+
+        x_rows = xT.rearrange("(p j) t -> p j t", j=4)
+        w1_rows = w1.rearrange("(p j) c -> p j c", j=4)
+        w2_rows = w2.rearrange("(p j) c -> p j c", j=4)
+
+        offs_sb = held.tile([P, S // 16], U16, name="offs_sb")
+        pos_sb = held.tile([P, S // 16], U16, name="pos_sb")
+        x_raw = []
+        for u, a, b in ((0, 0, 1024), (1, 0, 512), (1, 512, 1024)):
+            t = held.tile([P, 2, b - a], F32, name=f"x_raw{u}_{a}")
+            nc.sync.dma_start(out=t[:], in_=x_rows[:, 2 * u : 2 * u + 2, a:b])
+            x_raw.append(t)
+            if u == 0:
+                nc.sync.dma_start(offs_sb[:], offs)
+        w1_raw = []
+        for u in range(2):
+            t = held.tile([P, 2, H], F32, name=f"w1_raw{u}")
+            nc.sync.dma_start(out=t[:], in_=w1_rows[:, 2 * u : 2 * u + 2, :])
+            w1_raw.append(t)
+        gate_sb = held.tile([P, S], F32, name="gate_sb")
+        nc.sync.dma_start(out=gate_sb[:], in_=gate)
+        nc.sync.dma_start(pos_sb[:], pos1)
+        w2_raw = held.tile([P, 4, N], F32, name="w2_raw")
+        nc.sync.dma_start(out=w2_raw[:], in_=w2_rows)
+
+        warm = held.tile([P, 1], F32, name="warm")
+        warm_out = held.tile([P, 1], F32, name="warm_out")
+        nc.vector.memset(warm[:], 0.0)
+        nc.scalar.activation(warm_out[:], warm[:], SILU)
+
+        z = []
+        for t in range(4):
+            zt = held.tile([P, V], F32, name=f"z{t}")
+            nc.gpsimd.memset(zt[:], 0.0)
+            z.append(zt)
+
+        picked = held.tile([P, S, 4], BF16, name="picked", align_bytes=64)
+        picked_words = picked[:].rearrange("p s j -> p (s j)").bitcast(U32).rearrange("p (s u) -> p s u", u=2)
+        casts = (
+            (0, 0, 0, 0, 352, nc.scalar.copy),
+            (0, 0, 352, 352, 672, nc.vector.tensor_copy),
+            (1, 1, 0, 0, 512, nc.scalar.copy),
+            (1, 2, 0, 512, 352, nc.vector.tensor_copy),
+            (1, 2, 352, 864, 160, nc.scalar.copy),
+        )
+        for u in range(2):
+            pairs = held.tile([P, T, 2], BF16, name=f"pairs{u}", align_bytes=64)
+            for cu, raw, src, dst, n, cast in casts:
+                if cu == u:
+                    cast(
+                        out=pairs[:, dst : dst + n, :],
+                        in_=x_raw[raw][:, :, src : src + n].rearrange("p e t -> p t e"),
+                    )
+            window = pairs[:].rearrange("p t e -> p (t e)").bitcast(U32)
+            for b in range(2):
+                nc.vector.tensor_copy(
+                    out=picked_words[:, b * HALF : (b + 1) * HALF, u],
+                    in_=window.indirect(offs_sb[:, b * 16 : (b + 1) * 16]),
+                )
+        xq = held.tile([P, S], U32, name="xq", align_bytes=64)
+        xs = held.tile([P, S], U8, name="xs", align_bytes=64)
+        for b in range(2):
+            cols = slice(b * HALF, (b + 1) * HALF)
+            nc.vector.quantize_mx(
+                out=xq[:, cols].bitcast(FP8X4),
+                scales=xs[:, cols],
+                in_=picked[:, cols, :].rearrange("p s j -> p (s j)"),
+            )
+
+        w1_cols = []
+        for u in range(2):
+            w1_cols.append(w1_raw[u][:].rearrange("p e (m t) -> p t m e", t=4))
+        w1_grouped = held.tile([P, 4, 128, 4], BF16, name="w1_grouped", align_bytes=64)
+        w1q = held.tile([P, 4, 128], U32, name="w1q", align_bytes=64)
+        w1s = held.tile([P, 4, 128], U8, name="w1s", align_bytes=64)
+
+        def quantise_w1(t0, t1):
+            nc.vector.quantize_mx(
+                out=w1q[:, t0:t1, :].rearrange("p t m -> p (t m)").bitcast(FP8X4),
+                scales=w1s[:, t0:t1, :].rearrange("p t m -> p (t m)"),
+                in_=w1_grouped[:, t0:t1].rearrange("p t m j -> p (t m j)"),
+            )
+
+        def group_w1(t, u, copy):
+            copy(out=w1_grouped[:, t, :, 2 * u : 2 * u + 2], in_=w1_cols[u][:, t])
+
+        for t in range(4):
+            group_w1(t, 0, nc.scalar.copy)
+        group_w1(0, 1, nc.vector.tensor_copy)
+        group_w1(1, 1, nc.vector.tensor_copy)
+        quantise_w1(0, 1)
+        quantise_w1(1, 2)
+
+        def first_layer(t, cols):
+            bank = psum.tile([P, 512], F32, name="bank")
+            n = cols.stop - cols.start
+            nc.tensor.matmul_mx(
+                out=bank[:, 0:n],
+                lhsT=w1q[:, t, :].bitcast(FP8X4),
+                lhsT_scale=w1s[:, t, :],
+                rhs=xq[:, cols].bitcast(FP8X4),
+                rhs_scale=xs[:, cols],
+                start=True,
+                stop=True,
+            )
+            h = held.tile([P, n], F32, name=f"h{t}_{cols.start}")
+            nc.scalar.activation(h[:], bank[:, 0:n], SILU)
+            nc.vector.tensor_tensor(
+                z[t][:].indirect(pos_sb[:, cols.start // 16 : cols.stop // 16]), h[:], gate_sb[:, cols], MULT
+            )
+
+        zi = held.tile([P, V, 4], BF16, name="zi", align_bytes=64)
+        first_layer(0, slice(0, HALF))
+        first_layer(0, slice(HALF, S))
+        group_w1(2, 1, nc.scalar.copy)
+        group_w1(3, 1, nc.scalar.copy)
+        for t in range(1, 4):
+            if t == 2:
+                quantise_w1(2, 4)
+            first_layer(t, slice(0, S))
+            if t == 1:
+                w2_grouped = held.tile([P, N, 4], BF16, name="w2_grouped", align_bytes=64)
+                nc.scalar.copy(out=w2_grouped[:], in_=w2_raw[:].rearrange("p j m -> p m j"))
+                w2q = held.tile([P, N], U32, name="w2q", align_bytes=64)
+                w2s = held.tile([P, N], U8, name="w2s", align_bytes=64)
+                nc.vector.quantize_mx(
+                    out=w2q[:].bitcast(FP8X4), scales=w2s[:], in_=w2_grouped[:].rearrange("p m j -> p (m j)")
+                )
+        for t in range(2):
+            nc.scalar.copy(out=zi[:, :, t], in_=z[t][:])
+        for half in range(2):
+            cells = slice(half * 512, (half + 1) * 512)
+            nc.scalar.copy(out=zi[:, cells, 2:4], in_=z[2][:, cells].unsqueeze(2).to_broadcast([P, 512, 2]))
+
+        zq = held.tile([P, V], U32, name="zq", align_bytes=64)
+        zs = held.tile([P, V], U8, name="zs", align_bytes=64)
+        chunks = [slice(c * HALF, (c + 1) * HALF) for c in range(4)]
+        def slot3(a, b, copy):
+            copy(out=zi[:, a:b, 3], in_=z[3][:, a:b])
+
+        def quantise_z(c):
+            nc.vector.quantize_mx(
+                out=zq[:, chunks[c]].bitcast(FP8X4),
+                scales=zs[:, chunks[c]],
+                in_=zi[:, chunks[c], :].rearrange("p v j -> p (v j)"),
+            )
+
+        slot3(0, 256, nc.vector.tensor_copy)
+        slot3(512, 768, nc.scalar.copy)
+        slot3(768, 1024, nc.scalar.copy)
+        quantise_z(0)
+        slot3(256, 512, nc.vector.tensor_copy)
+        quantise_z(1)
+        quantise_z(2)
+        quantise_z(3)
+        out_rows = out.rearrange("(m p) v -> p m v", p=P)
+        for c in range(4):
+            res = held.tile([P, 2, HALF], F32, name=f"res{c}")
+            for m in range(2):
+                bank = psum.tile([P, 512], F32, name="bank")
+                nc.tensor.matmul_mx(
+                    out=bank[:, 0:HALF],
+                    lhsT=w2q[:, m * P : (m + 1) * P].bitcast(FP8X4),
+                    lhsT_scale=w2s[:, m * P : (m + 1) * P],
+                    rhs=zq[:, chunks[c]].bitcast(FP8X4),
+                    rhs_scale=zs[:, chunks[c]],
+                    start=True,
+                    stop=True,
+                )
+                copy = nc.vector.tensor_copy if c == 3 else nc.scalar.copy
+                copy(out=res[:, m, :], in_=bank[:, 0:HALF])
+                if c == 3:
+                    nc.sync.dma_start(out=out_rows[:, m, chunks[c]], in_=res[:, m, :])
+            if c < 3:
+                nc.sync.dma_start(out=out_rows[:, :, chunks[c]], in_=res[:])

@@ -31,20 +31,20 @@ def tile_picked_voxel_silu_e_kernel(tc, xT, w1, w2, gate, offs, pos1, out):
         offs_sb = held.tile([P, S // 16], U16, name="offs_sb")
         pos_sb = held.tile([P, S // 16], U16, name="pos_sb")
         x_raw = []
-        for u, a, b in ((0, 0, 1024), (1, 0, 512), (1, 512, 1024)):
-            t = held.tile([P, 2, b - a], F32, name=f"x_raw{u}_{a}")
-            nc.sync.dma_start(out=t[:], in_=x_rows[:, 2 * u : 2 * u + 2, a:b])
+        for j in range(4):
+            t = held.tile([P, T], F32, name=f"x_raw{j}")
+            nc.sync.dma_start(out=t[:], in_=x_rows[:, j, :])
             x_raw.append(t)
-            if u == 0:
+            if j == 0:
                 nc.sync.dma_start(offs_sb[:], offs)
         w1_raw = []
-        for u in range(2):
-            t = held.tile([P, 2, H], F32, name=f"w1_raw{u}")
-            nc.sync.dma_start(out=t[:], in_=w1_rows[:, 2 * u : 2 * u + 2, :])
+        for half in range(2):
+            t = held.tile([P, 4, HALF], F32, name=f"w1_raw{half}")
+            nc.sync.dma_start(out=t[:], in_=w1_rows[:, :, half * HALF : (half + 1) * HALF])
             w1_raw.append(t)
+        nc.sync.dma_start(pos_sb[:], pos1)
         gate_sb = held.tile([P, S], F32, name="gate_sb")
         nc.sync.dma_start(out=gate_sb[:], in_=gate)
-        nc.sync.dma_start(pos_sb[:], pos1)
         w2_raw = held.tile([P, 4, N], F32, name="w2_raw")
         nc.sync.dma_start(out=w2_raw[:], in_=w2_rows)
 
@@ -55,146 +55,170 @@ def tile_picked_voxel_silu_e_kernel(tc, xT, w1, w2, gate, offs, pos1, out):
 
         z = []
         for t in range(4):
-            zt = held.tile([P, V], F32, name=f"z{t}")
-            nc.gpsimd.memset(zt[:], 0.0)
+            zt = held.tile([P, V if t % 2 else 2 * V], F32, name=f"z{t}")
+            clear = nc.vector.memset if t % 2 else nc.gpsimd.memset
+            clear(zt[:, 0:V], 0.0)
             z.append(zt)
 
         picked = held.tile([P, S, 4], BF16, name="picked", align_bytes=64)
-        picked_words = picked[:].rearrange("p s j -> p (s j)").bitcast(U32).rearrange("p (s u) -> p s u", u=2)
-        casts = (
-            (0, 0, 0, 0, 352, nc.scalar.copy),
-            (0, 0, 352, 352, 672, nc.vector.tensor_copy),
-            (1, 1, 0, 0, 512, nc.scalar.copy),
-            (1, 2, 0, 512, 352, nc.vector.tensor_copy),
-            (1, 2, 352, 864, 160, nc.scalar.copy),
-        )
-        for u in range(2):
-            pairs = held.tile([P, T, 2], BF16, name=f"pairs{u}", align_bytes=64)
-            for cu, raw, src, dst, n, cast in casts:
-                if cu == u:
-                    cast(
-                        out=pairs[:, dst : dst + n, :],
-                        in_=x_raw[raw][:, :, src : src + n].rearrange("p e t -> p t e"),
-                    )
-            window = pairs[:].rearrange("p t e -> p (t e)").bitcast(U32)
-            for b in range(2):
-                nc.vector.tensor_copy(
-                    out=picked_words[:, b * HALF : (b + 1) * HALF, u],
-                    in_=window.indirect(offs_sb[:, b * 16 : (b + 1) * 16]),
-                )
-        xq = held.tile([P, S], U32, name="xq", align_bytes=64)
-        xs = held.tile([P, S], U8, name="xs", align_bytes=64)
-        for b in range(2):
-            cols = slice(b * HALF, (b + 1) * HALF)
-            nc.vector.quantize_mx(
-                out=xq[:, cols].bitcast(FP8X4),
-                scales=xs[:, cols],
-                in_=picked[:, cols, :].rearrange("p s j -> p (s j)"),
+        rows = [held.tile([P, 2, S], BF16, name=f"rows{u}") for u in range(2)]
+
+        def gather(j, a, b):
+            nc.vector.tensor_copy(
+                out=rows[j // 2][:, j % 2, a:b], in_=x_raw[j][:].indirect(offs_sb[:, a // 16 : b // 16])
             )
 
-        w1_cols = []
-        for u in range(2):
-            w1_cols.append(w1_raw[u][:].rearrange("p e (m t) -> p t m e", t=4))
+        def weave_points(u, a, b, copy):
+            copy(out=picked[:, a:b, 2 * u : 2 * u + 2], in_=rows[u][:, :, a:b].rearrange("p e s -> p s e"))
+
+        xq = held.tile([P, S], U32, name="xq", align_bytes=64)
+        xs = held.tile([P, S], U8, name="xs", align_bytes=64)
+
+        def quantise_points(a, b):
+            nc.vector.quantize_mx(
+                out=xq[:, a:b].bitcast(FP8X4),
+                scales=xs[:, a:b],
+                in_=picked[:, a:b, :].rearrange("p s j -> p (s j)"),
+            )
+
+        for j in range(3):
+            gather(j, 0, S)
+            if j == 1:
+                weave_points(0, 0, S, nc.scalar.copy)
+        gather(3, 0, HALF)
+        gather(3, HALF, S)
+        weave_points(1, 0, HALF, nc.vector.tensor_copy)
+        weave_points(1, HALF, S, nc.vector.tensor_copy)
+        quantise_points(0, HALF)
+        quantise_points(HALF, S)
+
+        order = (1, 3, 0, 2)
         w1_grouped = held.tile([P, 4, 128, 4], BF16, name="w1_grouped", align_bytes=64)
         w1q = held.tile([P, 4, 128], U32, name="w1q", align_bytes=64)
         w1s = held.tile([P, 4, 128], U8, name="w1s", align_bytes=64)
 
-        def quantise_w1(t0, t1):
-            nc.vector.quantize_mx(
-                out=w1q[:, t0:t1, :].rearrange("p t m -> p (t m)").bitcast(FP8X4),
-                scales=w1s[:, t0:t1, :].rearrange("p t m -> p (t m)"),
-                in_=w1_grouped[:, t0:t1].rearrange("p t m j -> p (t m j)"),
+        def group_w1(half, odd, copy):
+            r = 0 if odd else 2
+            copy(
+                out=w1_grouped[:, r : r + 2, half * 64 : (half + 1) * 64, :].rearrange("p u m j -> p m j u"),
+                in_=w1_raw[half][:].rearrange("p j (m u v) -> p v m j u", u=2, v=2)[:, odd],
             )
 
-        def group_w1(t, u, copy):
-            copy(out=w1_grouped[:, t, :, 2 * u : 2 * u + 2], in_=w1_cols[u][:, t])
+        def quantise_w1(r0, r1):
+            nc.vector.quantize_mx(
+                out=w1q[:, r0:r1, :].rearrange("p r m -> p (r m)").bitcast(FP8X4),
+                scales=w1s[:, r0:r1, :].rearrange("p r m -> p (r m)"),
+                in_=w1_grouped[:, r0:r1].rearrange("p r m j -> p (r m j)"),
+            )
 
-        for t in range(4):
-            group_w1(t, 0, nc.scalar.copy)
-        group_w1(0, 1, nc.vector.tensor_copy)
-        group_w1(1, 1, nc.vector.tensor_copy)
+        for half in range(2):
+            for odd in (1, 0):
+                group_w1(half, odd, nc.scalar.copy)
         quantise_w1(0, 1)
         quantise_w1(1, 2)
+        quantise_w1(2, 4)
 
-        def first_layer(t, cols):
+        def first_layer(r, edges):
             bank = psum.tile([P, 512], F32, name="bank")
-            n = cols.stop - cols.start
-            nc.tensor.matmul_mx(
-                out=bank[:, 0:n],
-                lhsT=w1q[:, t, :].bitcast(FP8X4),
-                lhsT_scale=w1s[:, t, :],
-                rhs=xq[:, cols].bitcast(FP8X4),
-                rhs_scale=xs[:, cols],
-                start=True,
-                stop=True,
-            )
-            h = held.tile([P, n], F32, name=f"h{t}_{cols.start}")
-            nc.scalar.activation(h[:], bank[:, 0:n], SILU)
-            nc.vector.tensor_tensor(
-                z[t][:].indirect(pos_sb[:, cols.start // 16 : cols.stop // 16]), h[:], gate_sb[:, cols], MULT
-            )
-
-        zi = held.tile([P, V, 4], BF16, name="zi", align_bytes=64)
-        first_layer(0, slice(0, HALF))
-        first_layer(0, slice(HALF, S))
-        group_w1(2, 1, nc.scalar.copy)
-        group_w1(3, 1, nc.scalar.copy)
-        for t in range(1, 4):
-            if t == 2:
-                quantise_w1(2, 4)
-            first_layer(t, slice(0, S))
-            if t == 1:
-                w2_grouped = held.tile([P, N, 4], BF16, name="w2_grouped", align_bytes=64)
-                nc.scalar.copy(out=w2_grouped[:], in_=w2_raw[:].rearrange("p j m -> p m j"))
-                w2q = held.tile([P, N], U32, name="w2q", align_bytes=64)
-                w2s = held.tile([P, N], U8, name="w2s", align_bytes=64)
-                nc.vector.quantize_mx(
-                    out=w2q[:].bitcast(FP8X4), scales=w2s[:], in_=w2_grouped[:].rearrange("p m j -> p (m j)")
-                )
-        for t in range(2):
-            nc.scalar.copy(out=zi[:, :, t], in_=z[t][:])
-        for half in range(2):
-            cells = slice(half * 512, (half + 1) * 512)
-            nc.scalar.copy(out=zi[:, cells, 2:4], in_=z[2][:, cells].unsqueeze(2).to_broadcast([P, 512, 2]))
-
-        zq = held.tile([P, V], U32, name="zq", align_bytes=64)
-        zs = held.tile([P, V], U8, name="zs", align_bytes=64)
-        chunks = [slice(c * HALF, (c + 1) * HALF) for c in range(4)]
-        def slot3(a, b, copy):
-            copy(out=zi[:, a:b, 3], in_=z[3][:, a:b])
-
-        def quantise_z(c):
-            nc.vector.quantize_mx(
-                out=zq[:, chunks[c]].bitcast(FP8X4),
-                scales=zs[:, chunks[c]],
-                in_=zi[:, chunks[c], :].rearrange("p v j -> p (v j)"),
-            )
-
-        slot3(0, 256, nc.vector.tensor_copy)
-        slot3(512, 768, nc.scalar.copy)
-        slot3(768, 1024, nc.scalar.copy)
-        quantise_z(0)
-        slot3(256, 512, nc.vector.tensor_copy)
-        quantise_z(1)
-        quantise_z(2)
-        quantise_z(3)
-        out_rows = out.rearrange("(m p) v -> p m v", p=P)
-        for c in range(4):
-            res = held.tile([P, 2, HALF], F32, name=f"res{c}")
-            for m in range(2):
-                bank = psum.tile([P, 512], F32, name="bank")
+            a, b = edges[0], edges[-1]
+            for c, d in zip(edges, edges[1:]):
                 nc.tensor.matmul_mx(
-                    out=bank[:, 0:HALF],
-                    lhsT=w2q[:, m * P : (m + 1) * P].bitcast(FP8X4),
-                    lhsT_scale=w2s[:, m * P : (m + 1) * P],
-                    rhs=zq[:, chunks[c]].bitcast(FP8X4),
-                    rhs_scale=zs[:, chunks[c]],
+                    out=bank[:, c - a : d - a],
+                    lhsT=w1q[:, r, :].bitcast(FP8X4),
+                    lhsT_scale=w1s[:, r, :],
+                    rhs=xq[:, c:d].bitcast(FP8X4),
+                    rhs_scale=xs[:, c:d],
                     start=True,
                     stop=True,
                 )
-                copy = nc.vector.tensor_copy if c == 3 else nc.scalar.copy
-                copy(out=res[:, m, :], in_=bank[:, 0:HALF])
-                if c == 3:
-                    nc.sync.dma_start(out=out_rows[:, m, chunks[c]], in_=res[:, m, :])
-            if c < 3:
-                nc.sync.dma_start(out=out_rows[:, :, chunks[c]], in_=res[:])
+            h = held.tile([P, b - a], F32, name=f"h{r}_{a}")
+            nc.scalar.activation(h[:], bank[:, 0 : b - a], SILU)
+            return h
+
+        def scatter(r, h, a, b):
+            nc.vector.tensor_tensor(
+                z[order[r]][:].indirect(pos_sb[:, a // 16 : b // 16]), h[:], gate_sb[:, a:b], MULT
+            )
+
+        for edges in ((0, 128), (128, 256, 512)):
+            for r in range(2):
+                scatter(r, first_layer(r, edges), edges[0], edges[-1])
+        h2 = first_layer(2, (0, S))
+        h3 = first_layer(3, (0, S))
+        nc.scalar.copy(out=z[0][:, V : 2 * V], in_=z[1][:])
+        scatter(2, h2, 0, S)
+        w2_grouped = held.tile([P, N, 4], BF16, name="w2_grouped", align_bytes=64)
+        nc.scalar.copy(out=w2_grouped[:], in_=w2_raw[:].rearrange("p j m -> p m j"))
+        w2q = held.tile([P, N], U32, name="w2q", align_bytes=64)
+        w2s = held.tile([P, N], U8, name="w2s", align_bytes=64)
+        nc.vector.quantize_mx(
+            out=w2q[:].bitcast(FP8X4), scales=w2s[:], in_=w2_grouped[:].rearrange("p m j -> p (m j)")
+        )
+        nc.scalar.copy(out=z[2][:, V : 2 * V], in_=z[3][:])
+        scatter(3, h3, 0, S)
+
+        zi = held.tile([P, V, 4], BF16, name="zi", align_bytes=64)
+
+        def weave_cells(u, a, b, copy):
+            copy(
+                out=zi[:, a:b, 2 * u : 2 * u + 2],
+                in_=z[2 * u][:].rearrange("p (e v) -> p v e", e=2)[:, a:b, :],
+            )
+
+        weave_cells(0, 0, 512, nc.scalar.copy)
+        weave_cells(0, 512, V, nc.scalar.copy)
+
+        zq = held.tile([P, V], U32, name="zq", align_bytes=64)
+        zs = held.tile([P, V], U8, name="zs", align_bytes=64)
+        chunks = ((0, 128), (128, 384), (384, 640), (640, 896), (896, 1024))
+
+        def quantise_z(c):
+            a, b = chunks[c]
+            nc.vector.quantize_mx(
+                out=zq[:, a:b].bitcast(FP8X4),
+                scales=zs[:, a:b],
+                in_=zi[:, a:b, :].rearrange("p v j -> p (v j)"),
+            )
+
+        weave_cells(1, *chunks[0], nc.vector.tensor_copy)
+        weave_cells(1, *chunks[1], nc.vector.tensor_copy)
+        weave_cells(1, *chunks[2], nc.scalar.copy)
+        weave_cells(1, *chunks[4], nc.scalar.copy)
+        quantise_z(0)
+        quantise_z(1)
+        weave_cells(1, *chunks[3], nc.vector.tensor_copy)
+        quantise_z(2)
+        quantise_z(3)
+        quantise_z(4)
+
+        out_rows = out.rearrange("(m p) v -> p m v", p=P)
+
+        def second_layer(dst, m, a, b):
+            nc.tensor.matmul_mx(
+                out=dst,
+                lhsT=w2q[:, m * P : (m + 1) * P].bitcast(FP8X4),
+                lhsT_scale=w2s[:, m * P : (m + 1) * P],
+                rhs=zq[:, a:b].bitcast(FP8X4),
+                rhs_scale=zs[:, a:b],
+                start=True,
+                stop=True,
+            )
+
+        for c, (a, b) in enumerate(chunks):
+            n = b - a
+            if n == 128:
+                res = held.tile([P, 2, n], F32, name=f"res{c}")
+                bank = psum.tile([P, 512], F32, name="bank")
+                for m in range(2):
+                    second_layer(bank[:, m * n : (m + 1) * n], m, a, b)
+                copy = nc.vector.tensor_copy if c == 4 else nc.scalar.copy
+                copy(out=res[:].rearrange("p m v -> p (m v)"), in_=bank[:, 0 : 2 * n])
+                nc.sync.dma_start(out=out_rows[:, :, a:b], in_=res[:])
+            else:
+                for m in range(2):
+                    res = held.tile([P, n], F32, name=f"res{c}_{m}")
+                    bank = psum.tile([P, 512], F32, name="bank")
+                    second_layer(bank[:, 0:n], m, a, b)
+                    copy = nc.vector.tensor_copy if (c, m) == (3, 1) else nc.scalar.copy
+                    copy(out=res[:], in_=bank[:, 0:n])
+                    nc.sync.dma_start(out=out_rows[:, m, a:b], in_=res[:])

@@ -55,7 +55,7 @@ def tile_picked_voxel_silu_e_kernel(tc, xT, w1, w2, gate, offs, pos1, out):
 
         z = []
         for t in range(4):
-            zt = held.tile([P, V if t % 2 else 2 * V], F32, name=f"z{t}")
+            zt = held.tile([P, V if t % 2 else 2 * V], F32, name=f"z{t}", tag=f"z{t}", align_bytes=64)
             clear = nc.vector.memset if t % 2 else nc.gpsimd.memset
             clear(zt[:, 0:V], 0.0)
             z.append(zt)
@@ -149,13 +149,13 @@ def tile_picked_voxel_silu_e_kernel(tc, xT, w1, w2, gate, offs, pos1, out):
         scatter(2, h2, 0, S)
         w2_grouped = held.tile([P, N, 4], BF16, name="w2_grouped", align_bytes=64)
         nc.scalar.copy(out=w2_grouped[:], in_=w2_raw[:].rearrange("p j m -> p m j"))
-        w2q = held.tile([P, N], U32, name="w2q", align_bytes=64)
+        nc.scalar.copy(out=z[2][:, V : 2 * V], in_=z[3][:])
+        scatter(3, h3, 0, S)
+        w2q = held.tile([P, N], U32, name="w2q", tag="z3", align_bytes=64)
         w2s = held.tile([P, N], U8, name="w2s", align_bytes=64)
         nc.vector.quantize_mx(
             out=w2q[:].bitcast(FP8X4), scales=w2s[:], in_=w2_grouped[:].rearrange("p m j -> p (m j)")
         )
-        nc.scalar.copy(out=z[2][:, V : 2 * V], in_=z[3][:])
-        scatter(3, h3, 0, S)
 
         zi = held.tile([P, V, 4], BF16, name="zi", align_bytes=64)
 
@@ -186,10 +186,10 @@ def tile_picked_voxel_silu_e_kernel(tc, xT, w1, w2, gate, offs, pos1, out):
         weave_cells(1, *chunks[4], nc.scalar.copy)
         quantise_z(0)
         quantise_z(1)
-        weave_cells(1, *chunks[3], nc.vector.tensor_copy)
         quantise_z(2)
-        quantise_z(3)
+        weave_cells(1, *chunks[3], nc.vector.tensor_copy)
         quantise_z(4)
+        quantise_z(3)
 
         out_rows = out.rearrange("(m p) v -> p m v", p=P)
 
@@ -206,19 +206,19 @@ def tile_picked_voxel_silu_e_kernel(tc, xT, w1, w2, gate, offs, pos1, out):
 
         for c, (a, b) in enumerate(chunks):
             n = b - a
-            if n == 128:
+            if c == 0:
                 res = held.tile([P, 2, n], F32, name=f"res{c}")
                 bank = psum.tile([P, 512], F32, name="bank")
                 for m in range(2):
                     second_layer(bank[:, m * n : (m + 1) * n], m, a, b)
-                copy = nc.vector.tensor_copy if c == 4 else nc.scalar.copy
-                copy(out=res[:].rearrange("p m v -> p (m v)"), in_=bank[:, 0 : 2 * n])
+                nc.scalar.copy(out=res[:].rearrange("p m v -> p (m v)"), in_=bank[:, 0 : 2 * n])
                 nc.sync.dma_start(out=out_rows[:, :, a:b], in_=res[:])
             else:
                 for m in range(2):
                     res = held.tile([P, n], F32, name=f"res{c}_{m}")
                     bank = psum.tile([P, 512], F32, name="bank")
                     second_layer(bank[:, 0:n], m, a, b)
-                    copy = nc.vector.tensor_copy if (c, m) == (3, 1) else nc.scalar.copy
+                    copy = nc.vector.tensor_copy if c >= 2 and m == 1 else nc.scalar.copy
                     copy(out=res[:], in_=bank[:, 0:n])
-                    nc.sync.dma_start(out=out_rows[:, m, a:b], in_=res[:])
+                    queue = nc.scalar if (c, m) == (4, 0) else nc.sync
+                    queue.dma_start(out=out_rows[:, m, a:b], in_=res[:])

@@ -26,7 +26,7 @@ def tile_picked_voxel_silu_e_kernel(tc, xT, w1, w2, gate, offs, pos1, out):
 
         x_rows = xT.rearrange("(p j) t -> p j t", j=4)
         w1_rows = w1.rearrange("(p j) c -> p j c", j=4)
-        w2_rows = w2.rearrange("(p j) c -> p j c", j=4)
+        w2_rows = w2.rearrange("(g t i) c -> t g i c", t=4, i=8)
 
         offs_sb = held.tile([P, S // 16], U16, name="offs_sb")
         pos_sb = held.tile([P, S // 16], U16, name="pos_sb")
@@ -37,16 +37,15 @@ def tile_picked_voxel_silu_e_kernel(tc, xT, w1, w2, gate, offs, pos1, out):
             x_raw.append(t)
             if j == 0:
                 nc.sync.dma_start(offs_sb[:], offs)
-        w1_raw = []
-        for half in range(2):
-            t = held.tile([P, 4, HALF], F32, name=f"w1_raw{half}")
-            nc.sync.dma_start(out=t[:], in_=w1_rows[:, :, half * HALF : (half + 1) * HALF])
-            w1_raw.append(t)
+        w1_raw = held.tile([P, 4, H], F32, name="w1_raw")
+        for e in (0, 2):
+            nc.sync.dma_start(out=w1_raw[:, e : e + 2, :], in_=w1_rows[:, e : e + 2, :])
         nc.sync.dma_start(pos_sb[:], pos1)
         gate_sb = held.tile([P, S], F32, name="gate_sb")
         nc.sync.dma_start(out=gate_sb[:], in_=gate)
         w2_raw = held.tile([P, 4, N], F32, name="w2_raw")
-        nc.sync.dma_start(out=w2_raw[:], in_=w2_rows)
+        for t in range(4):
+            nc.sync.dma_start(out=w2_raw[:, t, :], in_=w2_rows[t])
 
         warm = held.tile([P, 1], F32, name="warm")
         warm_out = held.tile([P, 1], F32, name="warm_out")
@@ -93,30 +92,30 @@ def tile_picked_voxel_silu_e_kernel(tc, xT, w1, w2, gate, offs, pos1, out):
         quantise_points(HALF, S)
 
         order = (1, 3, 0, 2)
-        w1_grouped = held.tile([P, 4, 128, 4], BF16, name="w1_grouped", align_bytes=64)
         w1q = held.tile([P, 4, 128], U32, name="w1q", align_bytes=64)
         w1s = held.tile([P, 4, 128], U8, name="w1s", align_bytes=64)
+        w1_from = w1_raw[:].rearrange("p j (g u v i) -> p v u g i j", u=2, v=2, i=8)
 
-        def group_w1(half, odd, copy):
-            r = 0 if odd else 2
-            copy(
-                out=w1_grouped[:, r : r + 2, half * 64 : (half + 1) * 64, :].rearrange("p u m j -> p m j u"),
-                in_=w1_raw[half][:].rearrange("p j (m u v) -> p v m j u", u=2, v=2)[:, odd],
-            )
-
-        def quantise_w1(r0, r1):
+        def quantise_w1(r0, r1, grouped):
             nc.vector.quantize_mx(
                 out=w1q[:, r0:r1, :].rearrange("p r m -> p (r m)").bitcast(FP8X4),
                 scales=w1s[:, r0:r1, :].rearrange("p r m -> p (r m)"),
-                in_=w1_grouped[:, r0:r1].rearrange("p r m j -> p (r m j)"),
+                in_=grouped,
             )
 
-        for half in range(2):
-            for odd in (1, 0):
-                group_w1(half, odd, nc.scalar.copy)
-        quantise_w1(0, 1)
-        quantise_w1(1, 2)
-        quantise_w1(2, 4)
+        odd = [held.tile([P, 128, 4], BF16, name=f"w1_odd{r}", tag=f"w1_odd{r}", align_bytes=64) for r in range(2)]
+        for e in (0, 2):
+            for r in range(2):
+                nc.scalar.copy(
+                    out=odd[r][:].rearrange("p (g i) j -> p g i j", i=8)[:, :, :, e : e + 2],
+                    in_=w1_from[:, 1, r, :, :, e : e + 2],
+                )
+        for r in range(2):
+            quantise_w1(r, r + 1, odd[r][:].rearrange("p m j -> p (m j)"))
+        for u, (copy, tag) in enumerate(((nc.scalar.copy, "w1_even"), (nc.vector.tensor_copy, "w1_odd0"))):
+            even = held.tile([P, 128, 4], BF16, name=f"w1_even{u}", tag=tag, align_bytes=64)
+            copy(out=even[:].rearrange("p (g i) j -> p g i j", i=8), in_=w1_from[:, 0, u])
+            quantise_w1(2 + u, 3 + u, even[:].rearrange("p m j -> p (m j)"))
 
         def first_layer(r, edges):
             bank = psum.tile([P, 512], F32, name="bank")

@@ -156,39 +156,48 @@ def tile_picked_voxel_silu_e_kernel(tc, xT, w1, w2, gate, offs, pos1, out):
             out=w2q[:].bitcast(FP8X4), scales=w2s[:], in_=w2_grouped[:].rearrange("p m j -> p (m j)")
         )
 
-        zi = held.tile([P, V, 4], BF16, name="zi", align_bytes=64)
+        chunks = ((0, 128), (128, 384), (384, 640), (640, 896), (896, 1024))
+        parts = ((0, 384), (384, 640), (640, 1024))
+        woven = [
+            held.tile([P, b - a, 4], BF16, name=f"woven{a}", tag=f"woven{a}", align_bytes=64) for a, b in parts
+        ]
+
+        def woven_cells(a, b):
+            for (start, stop), tile in zip(parts, woven):
+                if start <= a < stop:
+                    return tile[:, a - start : b - start, :]
 
         def weave_cells(u, a, b, copy):
             copy(
-                out=zi[:, a:b, 2 * u : 2 * u + 2],
+                out=woven_cells(a, b)[:, :, 2 * u : 2 * u + 2],
                 in_=z[2 * u][:].rearrange("p (e v) -> p v e", e=2)[:, a:b, :],
             )
 
-        weave_cells(0, 0, 512, nc.scalar.copy)
-        weave_cells(0, 512, V, nc.scalar.copy)
+        for a, b in parts:
+            weave_cells(0, a, b, nc.scalar.copy)
 
-        zq = held.tile([P, V], U32, name="zq", align_bytes=64)
         zs = held.tile([P, V], U8, name="zs", align_bytes=64)
-        chunks = ((0, 128), (128, 384), (384, 640), (640, 896), (896, 1024))
+        zq = {}
 
-        def quantise_z(c):
+        def quantise_z(c, tag):
             a, b = chunks[c]
+            zq[a] = held.tile([P, b - a], U32, name=f"zq{c}", tag=tag, align_bytes=64)
             nc.vector.quantize_mx(
-                out=zq[:, a:b].bitcast(FP8X4),
+                out=zq[a][:].bitcast(FP8X4),
                 scales=zs[:, a:b],
-                in_=zi[:, a:b, :].rearrange("p v j -> p (v j)"),
+                in_=woven_cells(a, b).rearrange("p v j -> p (v j)"),
             )
 
         weave_cells(1, *chunks[0], nc.vector.tensor_copy)
         weave_cells(1, *chunks[1], nc.vector.tensor_copy)
         weave_cells(1, *chunks[2], nc.scalar.copy)
         weave_cells(1, *chunks[4], nc.scalar.copy)
-        quantise_z(0)
-        quantise_z(1)
-        quantise_z(2)
+        quantise_z(0, "zq0")
+        quantise_z(1, "zq1")
         weave_cells(1, *chunks[3], nc.vector.tensor_copy)
-        quantise_z(4)
-        quantise_z(3)
+        quantise_z(2, "zq2")
+        quantise_z(3, "woven384")
+        quantise_z(4, "zq4")
 
         out_rows = out.rearrange("(m p) v -> p m v", p=P)
 
@@ -197,7 +206,7 @@ def tile_picked_voxel_silu_e_kernel(tc, xT, w1, w2, gate, offs, pos1, out):
                 out=dst,
                 lhsT=w2q[:, m * P : (m + 1) * P].bitcast(FP8X4),
                 lhsT_scale=w2s[:, m * P : (m + 1) * P],
-                rhs=zq[:, a:b].bitcast(FP8X4),
+                rhs=zq[a][:].bitcast(FP8X4),
                 rhs_scale=zs[:, a:b],
                 start=True,
                 stop=True,
@@ -205,19 +214,11 @@ def tile_picked_voxel_silu_e_kernel(tc, xT, w1, w2, gate, offs, pos1, out):
 
         for c, (a, b) in enumerate(chunks):
             n = b - a
-            if c == 0:
-                res = held.tile([P, 2, n], F32, name=f"res{c}")
+            for m in range(2):
+                res = held.tile([P, n], F32, name=f"res{c}_{m}")
                 bank = psum.tile([P, 512], F32, name="bank")
-                for m in range(2):
-                    second_layer(bank[:, m * n : (m + 1) * n], m, a, b)
-                nc.scalar.copy(out=res[:].rearrange("p m v -> p (m v)"), in_=bank[:, 0 : 2 * n])
-                nc.sync.dma_start(out=out_rows[:, :, a:b], in_=res[:])
-            else:
-                for m in range(2):
-                    res = held.tile([P, n], F32, name=f"res{c}_{m}")
-                    bank = psum.tile([P, 512], F32, name="bank")
-                    second_layer(bank[:, 0:n], m, a, b)
-                    copy = nc.vector.tensor_copy if c >= 2 and m == 1 else nc.scalar.copy
-                    copy(out=res[:], in_=bank[:, 0:n])
-                    queue = nc.scalar if (c, m) == (4, 0) else nc.sync
-                    queue.dma_start(out=out_rows[:, m, a:b], in_=res[:])
+                second_layer(bank[:, 0:n], m, a, b)
+                copy = nc.vector.tensor_copy if c >= 2 and m == 1 else nc.scalar.copy
+                copy(out=res[:], in_=bank[:, 0:n])
+                queue = nc.scalar if (c, m) == (4, 0) else nc.sync
+                queue.dma_start(out=out_rows[:, m, a:b], in_=res[:])

@@ -114,7 +114,10 @@ def tile_picked_voxel_silu_e_kernel(tc, xT, w1, w2, gate, offs, pos1, out):
             quantise_w1(r, r + 1, odd[r][:].rearrange("p m j -> p (m j)"))
         for u, (copy, tag) in enumerate(((nc.scalar.copy, "w1_even"), (nc.vector.tensor_copy, "w1_odd0"))):
             even = held.tile([P, 128, 4], BF16, name=f"w1_even{u}", tag=tag, align_bytes=64)
-            copy(out=even[:].rearrange("p (g i) j -> p g i j", i=8), in_=w1_from[:, 0, u])
+            copy(
+                out=even[:].rearrange("p (g h i) j -> p g h j i", h=2, i=4),
+                in_=w1_from[:, 0, u].rearrange("p g (h i) j -> p g h j i", i=4),
+            )
             quantise_w1(2 + u, 3 + u, even[:].rearrange("p m j -> p (m j)"))
 
         def first_layer(r, edges):
@@ -214,11 +217,13 @@ def tile_picked_voxel_silu_e_kernel(tc, xT, w1, w2, gate, offs, pos1, out):
 
         for c, (a, b) in enumerate(chunks):
             n = b - a
+            res = held.tile([P, 2, n], F32, name=f"res{c}")
             for m in range(2):
-                res = held.tile([P, n], F32, name=f"res{c}_{m}")
                 bank = psum.tile([P, 512], F32, name="bank")
                 second_layer(bank[:, 0:n], m, a, b)
                 copy = nc.vector.tensor_copy if c >= 2 and m == 1 else nc.scalar.copy
-                copy(out=res[:], in_=bank[:, 0:n])
-                queue = nc.scalar if (c, m) == (4, 0) else nc.sync
-                queue.dma_start(out=out_rows[:, m, a:b], in_=res[:])
+                copy(out=res[:, m, :], in_=bank[:, 0:n])
+                if n == 256:
+                    nc.sync.dma_start(out=out_rows[:, m, a:b], in_=res[:, m, :])
+            if n == 128:
+                nc.sync.dma_start(out=out_rows[:, :, a:b], in_=res[:])

@@ -55,9 +55,10 @@ def tile_picked_voxel_silu_e_kernel(tc, xT, w1, w2, gate, offs, pos1, out):
         z = []
         for t in range(4):
             zt = held.tile([P, V if t % 2 else 2 * V], F32, name=f"z{t}", tag=f"z{t}", align_bytes=64)
-            clear = nc.vector.memset if t % 2 else nc.gpsimd.memset
-            clear(zt[:, 0:V], 0.0)
             z.append(zt)
+        for t in (1, 3):
+            nc.vector.memset(z[t][:], 0.0)
+            nc.scalar.copy(out=z[t - 1][:, 0:V], in_=z[t][:])
 
         picked = held.tile([P, S, 4], BF16, name="picked", align_bytes=64)
         rows = [held.tile([P, 2, S], BF16, name=f"rows{u}") for u in range(2)]

@@ -12,6 +12,7 @@ U16 = mybir.dt.uint16
 U8 = mybir.dt.uint8
 FP8X4 = mybir.dt.float8_e4m3fn_x4
 SILU = mybir.ActivationFunctionType.Silu
+COPY = mybir.ActivationFunctionType.Copy
 MULT = mybir.AluOpType.mult
 
 P = 128
@@ -37,9 +38,11 @@ def tile_picked_voxel_silu_e_kernel(tc, xT, w1, w2, gate, offs, pos1, out):
             x_raw.append(t)
             if j == 0:
                 nc.sync.dma_start(offs_sb[:], offs)
-        w1_raw = held.tile([P, 4, H], F32, name="w1_raw")
-        for e in (0, 2):
-            nc.sync.dma_start(out=w1_raw[:, e : e + 2, :], in_=w1_rows[:, e : e + 2, :])
+        w1_raw = []
+        for u in range(2):
+            t = held.tile([P, 2, H], F32, name=f"w1_raw{u}")
+            nc.sync.dma_start(out=t[:], in_=w1_rows[:, 2 * u : 2 * u + 2, :])
+            w1_raw.append(t)
         nc.sync.dma_start(pos_sb[:], pos1)
         gate_sb = held.tile([P, S], F32, name="gate_sb")
         nc.sync.dma_start(out=gate_sb[:], in_=gate)
@@ -52,177 +55,139 @@ def tile_picked_voxel_silu_e_kernel(tc, xT, w1, w2, gate, offs, pos1, out):
         nc.vector.memset(warm[:], 0.0)
         nc.scalar.activation(warm_out[:], warm[:], SILU)
 
-        z = []
-        for t in range(4):
-            zt = held.tile([P, V if t % 2 else 2 * V], F32, name=f"z{t}", tag=f"z{t}", align_bytes=64)
-            z.append(zt)
-        for t in (1, 3):
-            nc.vector.memset(z[t][:], 0.0)
-            nc.scalar.copy(out=z[t - 1][:, 0:V], in_=z[t][:])
+        z = [held.tile([P, V if t % 2 else 2 * V], F32, name=f"z{t}") for t in range(4)]
+        for t in (1, 3, 2, 0):
+            nc.vector.memset(z[t][:, 0:V], 0.0)
 
-        picked = held.tile([P, S, 4], BF16, name="picked", align_bytes=64)
-        rows = [held.tile([P, 2, S], BF16, name=f"rows{u}") for u in range(2)]
-
-        def gather(j, a, b):
-            nc.vector.tensor_copy(
-                out=rows[j // 2][:, j % 2, a:b], in_=x_raw[j][:].indirect(offs_sb[:, a // 16 : b // 16])
-            )
-
-        def weave_points(u, a, b, copy):
-            copy(out=picked[:, a:b, 2 * u : 2 * u + 2], in_=rows[u][:, :, a:b].rearrange("p e s -> p s e"))
-
+        picked = [held.tile([P, HALF, 4], BF16, name=f"picked{e}", align_bytes=64) for e in range(2)]
+        for j in range(4):
+            nc.vector.tensor_copy(out=picked[0][:, :, j], in_=x_raw[j][:].indirect(offs_sb[:, 0:16]))
+            nc.scalar.activation(picked[1][:, :, j], x_raw[j][:].indirect(offs_sb[:, 16:32]), COPY)
         xq = held.tile([P, S], U32, name="xq", align_bytes=64)
         xs = held.tile([P, S], U8, name="xs", align_bytes=64)
-
-        def quantise_points(a, b):
+        for e in (1, 0):
             nc.vector.quantize_mx(
-                out=xq[:, a:b].bitcast(FP8X4),
-                scales=xs[:, a:b],
-                in_=picked[:, a:b, :].rearrange("p s j -> p (s j)"),
+                out=xq[:, e * HALF : (e + 1) * HALF].bitcast(FP8X4),
+                scales=xs[:, e * HALF : (e + 1) * HALF],
+                in_=picked[e][:].rearrange("p s j -> p (s j)"),
             )
 
-        for j in range(3):
-            gather(j, 0, S)
-            if j == 1:
-                weave_points(0, 0, S, nc.scalar.copy)
-        gather(3, 0, HALF)
-        gather(3, HALF, S)
-        weave_points(1, 0, HALF, nc.vector.tensor_copy)
-        weave_points(1, HALF, S, nc.vector.tensor_copy)
-        quantise_points(0, HALF)
-        quantise_points(HALF, S)
-
-        order = (1, 3, 0, 2)
         w1q = held.tile([P, 4, 128], U32, name="w1q", align_bytes=64)
         w1s = held.tile([P, 4, 128], U8, name="w1s", align_bytes=64)
-        w1_from = w1_raw[:].rearrange("p j (g u v i) -> p v u g i j", u=2, v=2, i=8)
-
-        def quantise_w1(r0, r1, grouped):
-            nc.vector.quantize_mx(
-                out=w1q[:, r0:r1, :].rearrange("p r m -> p (r m)").bitcast(FP8X4),
-                scales=w1s[:, r0:r1, :].rearrange("p r m -> p (r m)"),
-                in_=grouped,
-            )
-
-        odd = [held.tile([P, 128, 4], BF16, name=f"w1_odd{r}", tag=f"w1_odd{r}", align_bytes=64) for r in range(2)]
-        for e in (0, 2):
-            for r in range(2):
-                nc.scalar.copy(
-                    out=odd[r][:].rearrange("p (g i) j -> p g i j", i=8)[:, :, :, e : e + 2],
-                    in_=w1_from[:, 1, r, :, :, e : e + 2],
+        grouped = [held.tile([P, 128, 4], BF16, name=f"w1_grouped{t}", align_bytes=64) for t in range(4)]
+        for u in range(2):
+            w1_from = w1_raw[u][:].rearrange("p e (g t i) -> p t g i e", t=4, i=8)
+            for t, copy in ((1, nc.vector.tensor_copy), (3, nc.scalar.copy), (2, nc.vector.tensor_copy), (0, nc.scalar.copy)):
+                copy(
+                    out=grouped[t][:].rearrange("p (g i) j -> p g i j", i=8)[:, :, :, 2 * u : 2 * u + 2],
+                    in_=w1_from[:, t],
                 )
-        for r in range(2):
-            quantise_w1(r, r + 1, odd[r][:].rearrange("p m j -> p (m j)"))
-        for u, (copy, tag) in enumerate(((nc.scalar.copy, "w1_even"), (nc.vector.tensor_copy, "w1_odd0"))):
-            even = held.tile([P, 128, 4], BF16, name=f"w1_even{u}", tag=tag, align_bytes=64)
-            copy(
-                out=even[:].rearrange("p (g h i) j -> p g h j i", h=2, i=4),
-                in_=w1_from[:, 0, u].rearrange("p g (h i) j -> p g h j i", i=4),
+        for t in (1, 3, 2, 0):
+            nc.vector.quantize_mx(
+                out=w1q[:, t, :].bitcast(FP8X4), scales=w1s[:, t, :], in_=grouped[t][:].rearrange("p m j -> p (m j)")
             )
-            quantise_w1(2 + u, 3 + u, even[:].rearrange("p m j -> p (m j)"))
 
-        def first_layer(r, edges):
+        h = [held.tile([P, S], F32, name=f"h{t}") for t in range(4)]
+        gated = {t: held.tile([P, S], F32, name=f"gated{t}") for t in (3, 0)}
+
+        def first_layer(t, edges):
             bank = psum.tile([P, 512], F32, name="bank")
             a, b = edges[0], edges[-1]
             for c, d in zip(edges, edges[1:]):
                 nc.tensor.matmul_mx(
                     out=bank[:, c - a : d - a],
-                    lhsT=w1q[:, r, :].bitcast(FP8X4),
-                    lhsT_scale=w1s[:, r, :],
+                    lhsT=w1q[:, t, :].bitcast(FP8X4),
+                    lhsT_scale=w1s[:, t, :],
                     rhs=xq[:, c:d].bitcast(FP8X4),
                     rhs_scale=xs[:, c:d],
                     start=True,
                     stop=True,
                 )
-            h = held.tile([P, b - a], F32, name=f"h{r}_{a}")
-            nc.scalar.activation(h[:], bank[:, 0 : b - a], SILU)
-            return h
+            nc.scalar.activation(h[t][:, a:b], bank[:, 0 : b - a], SILU)
 
-        def scatter(r, h, a, b):
-            nc.vector.tensor_tensor(
-                z[order[r]][:].indirect(pos_sb[:, a // 16 : b // 16]), h[:], gate_sb[:, a:b], MULT
-            )
+        def scatter_on_vector(t, a, b):
+            nc.vector.tensor_tensor(z[t][:].indirect(pos_sb[:, a // 16 : b // 16]), h[t][:, a:b], gate_sb[:, a:b], MULT)
 
-        for edges in ((0, 128), (128, 256, 512)):
-            for r in range(2):
-                scatter(r, first_layer(r, edges), edges[0], edges[-1])
-        h2 = first_layer(2, (0, S))
-        h3 = first_layer(3, (0, S))
-        nc.scalar.copy(out=z[0][:, V : 2 * V], in_=z[1][:])
-        scatter(2, h2, 0, S)
+        def weigh(t, a, b):
+            nc.vector.tensor_tensor(gated[t][:, a:b], h[t][:, a:b], gate_sb[:, a:b], MULT)
+
+        def scatter_on_scalar(t, a, b):
+            nc.scalar.activation(z[t][:].indirect(pos_sb[:, a // 16 : b // 16]), gated[t][:, a:b], COPY)
+
+        first_layer(1, (0, 128))
+        first_layer(3, (0, HALF))
+        first_layer(3, (HALF, S))
+        first_layer(1, (128, 256, S))
+        first_layer(2, (0, S))
+        scatter_on_vector(1, 0, 128)
+        weigh(3, 0, S)
+        scatter_on_vector(1, 128, S)
+        nc.sync.dma_start(out=z[0][:, V : 2 * V], in_=z[1][:])
+        scatter_on_scalar(3, 0, HALF)
+        first_layer(0, (0, S))
+        scatter_on_scalar(3, HALF, S)
+        scatter_on_vector(2, 0, HALF)
+        weigh(0, 0, S)
+        nc.vector.tensor_copy(out=z[2][:, V : 2 * V], in_=z[3][:])
         w2_grouped = held.tile([P, N, 4], BF16, name="w2_grouped", align_bytes=64)
         nc.scalar.copy(out=w2_grouped[:], in_=w2_raw[:].rearrange("p j m -> p m j"))
-        nc.scalar.copy(out=z[2][:, V : 2 * V], in_=z[3][:])
-        scatter(3, h3, 0, S)
-        w2q = held.tile([P, N], U32, name="w2q", tag="z3", align_bytes=64)
+        w2q = held.tile([P, N], U32, name="w2q", align_bytes=64)
         w2s = held.tile([P, N], U8, name="w2s", align_bytes=64)
         nc.vector.quantize_mx(
             out=w2q[:].bitcast(FP8X4), scales=w2s[:], in_=w2_grouped[:].rearrange("p m j -> p (m j)")
         )
+        scatter_on_vector(2, HALF, S)
+        scatter_on_scalar(0, 0, HALF)
+        scatter_on_scalar(0, HALF, S)
 
         chunks = ((0, 128), (128, 384), (384, 640), (640, 896), (896, 1024))
-        parts = ((0, 384), (384, 640), (640, 1024))
-        woven = [
-            held.tile([P, b - a, 4], BF16, name=f"woven{a}", tag=f"woven{a}", align_bytes=64) for a, b in parts
-        ]
+        woven = [held.tile([P, b - a, 4], BF16, name=f"woven{a}", align_bytes=64) for a, b in chunks]
 
-        def woven_cells(a, b):
-            for (start, stop), tile in zip(parts, woven):
-                if start <= a < stop:
-                    return tile[:, a - start : b - start, :]
-
-        def weave_cells(u, a, b, copy):
+        def weave_cells(u, c, copy):
+            a, b = chunks[c]
             copy(
-                out=woven_cells(a, b)[:, :, 2 * u : 2 * u + 2],
+                out=woven[c][:, :, 2 * u : 2 * u + 2],
                 in_=z[2 * u][:].rearrange("p (e v) -> p v e", e=2)[:, a:b, :],
             )
 
-        for a, b in parts:
-            weave_cells(0, a, b, nc.scalar.copy)
-
         zs = held.tile([P, V], U8, name="zs", align_bytes=64)
-        zq = {}
+        zq = held.tile([P, V], U32, name="zq", align_bytes=64)
 
-        def quantise_z(c, tag):
+        def quantise_z(c):
             a, b = chunks[c]
-            zq[a] = held.tile([P, b - a], U32, name=f"zq{c}", tag=tag, align_bytes=64)
             nc.vector.quantize_mx(
-                out=zq[a][:].bitcast(FP8X4),
-                scales=zs[:, a:b],
-                in_=woven_cells(a, b).rearrange("p v j -> p (v j)"),
+                out=zq[:, a:b].bitcast(FP8X4), scales=zs[:, a:b], in_=woven[c][:].rearrange("p v j -> p (v j)")
             )
 
-        weave_cells(1, *chunks[0], nc.vector.tensor_copy)
-        weave_cells(1, *chunks[1], nc.vector.tensor_copy)
-        weave_cells(1, *chunks[2], nc.scalar.copy)
-        weave_cells(1, *chunks[4], nc.scalar.copy)
-        quantise_z(0, "zq0")
-        quantise_z(1, "zq1")
-        weave_cells(1, *chunks[3], nc.vector.tensor_copy)
-        quantise_z(2, "zq2")
-        quantise_z(3, "woven384")
-        quantise_z(4, "zq4")
+        for c in range(5):
+            weave_cells(1, c, nc.vector.tensor_copy)
+        weave_cells(0, 0, nc.vector.tensor_copy)
+        weave_cells(0, 1, nc.vector.tensor_copy)
+        weave_cells(0, 2, nc.scalar.copy)
+        quantise_z(0)
+        quantise_z(1)
+        weave_cells(0, 3, nc.vector.tensor_copy)
+        quantise_z(2)
+        weave_cells(0, 4, nc.vector.tensor_copy)
+        quantise_z(3)
+        quantise_z(4)
 
         out_rows = out.rearrange("(m p) v -> p m v", p=P)
-
-        def second_layer(dst, m, a, b):
-            nc.tensor.matmul_mx(
-                out=dst,
-                lhsT=w2q[:, m * P : (m + 1) * P].bitcast(FP8X4),
-                lhsT_scale=w2s[:, m * P : (m + 1) * P],
-                rhs=zq[a][:].bitcast(FP8X4),
-                rhs_scale=zs[:, a:b],
-                start=True,
-                stop=True,
-            )
-
         for c, (a, b) in enumerate(chunks):
             n = b - a
             res = held.tile([P, 2, n], F32, name=f"res{c}")
             for m in range(2):
                 bank = psum.tile([P, 512], F32, name="bank")
-                second_layer(bank[:, 0:n], m, a, b)
-                copy = nc.vector.tensor_copy if c >= 2 and m == 1 else nc.scalar.copy
+                nc.tensor.matmul_mx(
+                    out=bank[:, 0:n],
+                    lhsT=w2q[:, m * P : (m + 1) * P].bitcast(FP8X4),
+                    lhsT_scale=w2s[:, m * P : (m + 1) * P],
+                    rhs=zq[:, a:b].bitcast(FP8X4),
+                    rhs_scale=zs[:, a:b],
+                    start=True,
+                    stop=True,
+                )
+                copy = nc.vector.tensor_copy if c >= 3 and m == 1 else nc.scalar.copy
                 copy(out=res[:, m, :], in_=bank[:, 0:n])
                 if n == 256:
                     nc.sync.dma_start(out=out_rows[:, m, a:b], in_=res[:, m, :])

@@ -55,9 +55,9 @@ def tile_picked_voxel_silu_e_kernel(tc, xT, w1, w2, gate, offs, pos1, out):
         nc.vector.memset(warm[:], 0.0)
         nc.scalar.activation(warm_out[:], warm[:], SILU)
 
-        z = [held.tile([P, V if t % 2 else 2 * V], F32, name=f"z{t}") for t in range(4)]
-        for t in (1, 3, 2, 0):
-            nc.vector.memset(z[t][:, 0:V], 0.0)
+        z = [held.tile([P, V], F32, name=f"z{t}") for t in range(4)]
+        for t in range(4):
+            nc.vector.memset(z[t][:], 0.0)
 
         picked = [held.tile([P, HALF, 4], BF16, name=f"picked{e}", align_bytes=64) for e in range(2)]
         for j in range(4):
@@ -77,119 +77,127 @@ def tile_picked_voxel_silu_e_kernel(tc, xT, w1, w2, gate, offs, pos1, out):
         grouped = [held.tile([P, 128, 4], BF16, name=f"w1_grouped{t}", align_bytes=64) for t in range(4)]
         for u in range(2):
             w1_from = w1_raw[u][:].rearrange("p e (g t i) -> p t g i e", t=4, i=8)
-            for t, copy in ((1, nc.vector.tensor_copy), (3, nc.scalar.copy), (2, nc.vector.tensor_copy), (0, nc.scalar.copy)):
+            for t, copy in ((1, nc.vector.tensor_copy), (3, nc.scalar.copy), (0, nc.vector.tensor_copy), (2, nc.scalar.copy)):
                 copy(
                     out=grouped[t][:].rearrange("p (g i) j -> p g i j", i=8)[:, :, :, 2 * u : 2 * u + 2],
                     in_=w1_from[:, t],
                 )
-        for t in (1, 3, 2, 0):
+        for t in (1, 0, 3, 2):
             nc.vector.quantize_mx(
                 out=w1q[:, t, :].bitcast(FP8X4), scales=w1s[:, t, :], in_=grouped[t][:].rearrange("p m j -> p (m j)")
             )
 
-        h = [held.tile([P, S], F32, name=f"h{t}") for t in range(4)]
-        gated = {t: held.tile([P, S], F32, name=f"gated{t}") for t in (3, 0)}
-
-        def first_layer(t, edges):
+        def first_layer(dst, pieces):
             bank = psum.tile([P, 512], F32, name="bank")
-            a, b = edges[0], edges[-1]
-            for c, d in zip(edges, edges[1:]):
+            at = 0
+            for t, a, b in pieces:
                 nc.tensor.matmul_mx(
-                    out=bank[:, c - a : d - a],
+                    out=bank[:, at : at + b - a],
                     lhsT=w1q[:, t, :].bitcast(FP8X4),
                     lhsT_scale=w1s[:, t, :],
-                    rhs=xq[:, c:d].bitcast(FP8X4),
-                    rhs_scale=xs[:, c:d],
+                    rhs=xq[:, a:b].bitcast(FP8X4),
+                    rhs_scale=xs[:, a:b],
                     start=True,
                     stop=True,
                 )
-            nc.scalar.activation(h[t][:, a:b], bank[:, 0 : b - a], SILU)
+                at = at + b - a
+            nc.scalar.activation(dst, bank[:, 0:at], SILU)
 
-        def scatter_on_vector(t, a, b):
-            nc.vector.tensor_tensor(z[t][:].indirect(pos_sb[:, a // 16 : b // 16]), h[t][:, a:b], gate_sb[:, a:b], MULT)
+        def cells(t, a, b):
+            return z[t][:].indirect(pos_sb[:, a // 16 : b // 16])
+
+        h = [held.tile([P, S], F32, name=f"h{t}", tag=f"h{t}", align_bytes=64) for t in range(4)]
+        gated = {t: held.tile([P, S], F32, name=f"gated{t}") for t in (1, 3)}
+
+        def plane_layer(t, edges):
+            first_layer(h[t][:, edges[0] : edges[-1]], [(t, a, b) for a, b in zip(edges, edges[1:])])
 
         def weigh(t, a, b):
             nc.vector.tensor_tensor(gated[t][:, a:b], h[t][:, a:b], gate_sb[:, a:b], MULT)
 
-        def scatter_on_scalar(t, a, b):
-            nc.scalar.activation(z[t][:].indirect(pos_sb[:, a // 16 : b // 16]), gated[t][:, a:b], COPY)
+        def scatter_on_vector(t, a, b):
+            nc.vector.tensor_tensor(cells(t, a, b), h[t][:, a:b], gate_sb[:, a:b], MULT)
 
-        first_layer(1, (0, 128))
-        first_layer(3, (0, HALF))
-        first_layer(3, (HALF, S))
-        first_layer(1, (128, 256, S))
-        first_layer(2, (0, S))
-        scatter_on_vector(1, 0, 128)
+        def scatter_on_scalar(t, a, b):
+            nc.scalar.activation(cells(t, a, b), gated[t][:, a:b], COPY)
+
+        parts = ((0, HALF), (HALF, V))
+        planes = [held.tile([P, 4 * (b - a)], F32, name=f"planes{a}") for a, b in parts]
+
+        def plane_cells(a, b):
+            for (start, stop), tile in zip(parts, planes):
+                if start <= a < stop:
+                    return tile[:].rearrange("p (t v) -> p t v", t=4)[:, :, a - start : b - start]
+
+        plane_layer(1, (0, HALF))
+        plane_layer(0, (0, 128))
+        plane_layer(1, (HALF, S))
+        plane_layer(0, (128, 256, S))
+        weigh(1, 0, HALF)
+        scatter_on_vector(0, 0, 128)
+        weigh(1, HALF, S)
+        scatter_on_vector(0, 128, S)
+        for a, b in parts:
+            nc.sync.dma_start(out=plane_cells(a, b)[:, 0, :], in_=z[0][:, a:b])
+        scatter_on_scalar(1, 0, HALF)
+        plane_layer(3, (0, S))
+        plane_layer(2, (0, S))
+        scatter_on_scalar(1, HALF, S)
+        for a, b in parts:
+            nc.sync.dma_start(out=plane_cells(a, b)[:, 1, :], in_=z[1][:, a:b])
         weigh(3, 0, S)
-        scatter_on_vector(1, 128, S)
-        nc.sync.dma_start(out=z[0][:, V : 2 * V], in_=z[1][:])
+        scatter_on_vector(2, 0, S)
+        w2_grouped = held.tile([P, N, 4], BF16, name="w2_grouped", tag="h3", align_bytes=64)
+        w2_from = w2_raw[:].rearrange("p j m -> p m j")
         scatter_on_scalar(3, 0, HALF)
-        first_layer(0, (0, S))
+        nc.scalar.copy(out=w2_grouped[:, 0:64, :], in_=w2_from[:, 0:64, :])
         scatter_on_scalar(3, HALF, S)
-        scatter_on_vector(2, 0, HALF)
-        weigh(0, 0, S)
-        nc.vector.tensor_copy(out=z[2][:, V : 2 * V], in_=z[3][:])
-        w2_grouped = held.tile([P, N, 4], BF16, name="w2_grouped", align_bytes=64)
-        nc.scalar.copy(out=w2_grouped[:], in_=w2_raw[:].rearrange("p j m -> p m j"))
+        nc.vector.tensor_copy(out=w2_grouped[:, 64:N, :], in_=w2_from[:, 64:N, :])
+        nc.vector.tensor_copy(out=plane_cells(*parts[0])[:, 2, :], in_=z[2][:, 0:HALF])
         w2q = held.tile([P, N], U32, name="w2q", align_bytes=64)
         w2s = held.tile([P, N], U8, name="w2s", align_bytes=64)
         nc.vector.quantize_mx(
             out=w2q[:].bitcast(FP8X4), scales=w2s[:], in_=w2_grouped[:].rearrange("p m j -> p (m j)")
         )
-        scatter_on_vector(2, HALF, S)
-        scatter_on_scalar(0, 0, HALF)
-        scatter_on_scalar(0, HALF, S)
 
-        chunks = ((0, 128), (128, 384), (384, 640), (640, 896), (896, 1024))
-        woven = [held.tile([P, b - a, 4], BF16, name=f"woven{a}", align_bytes=64) for a, b in chunks]
+        nc.vector.tensor_copy(out=plane_cells(*parts[1])[:, 2, :], in_=z[2][:, HALF:V])
+        for a, b in ((0, 128), (128, HALF), (HALF, 512), (512, V)):
+            nc.scalar.copy(out=plane_cells(a, b)[:, 3, :], in_=z[3][:, a:b])
 
-        def weave_cells(u, c, copy):
-            a, b = chunks[c]
-            copy(
-                out=woven[c][:, :, 2 * u : 2 * u + 2],
-                in_=z[2 * u][:].rearrange("p (e v) -> p v e", e=2)[:, a:b, :],
-            )
-
+        woven = [held.tile([P, 128, 4], BF16, name=f"woven{c}", align_bytes=64) for c in range(8)]
         zs = held.tile([P, V], U8, name="zs", align_bytes=64)
         zq = held.tile([P, V], U32, name="zq", align_bytes=64)
 
-        def quantise_z(c):
-            a, b = chunks[c]
-            nc.vector.quantize_mx(
-                out=zq[:, a:b].bitcast(FP8X4), scales=zs[:, a:b], in_=woven[c][:].rearrange("p v j -> p (v j)")
+        def weave_cells(c, copy):
+            copy(
+                out=woven[c][:].rearrange("p (w i) t -> p w t i", i=4),
+                in_=plane_cells(128 * c, 128 * (c + 1)).rearrange("p t (w i) -> p w t i", i=4),
             )
 
-        for c in range(5):
-            weave_cells(1, c, nc.vector.tensor_copy)
-        weave_cells(0, 0, nc.vector.tensor_copy)
-        weave_cells(0, 1, nc.vector.tensor_copy)
-        weave_cells(0, 2, nc.scalar.copy)
-        quantise_z(0)
-        quantise_z(1)
-        weave_cells(0, 3, nc.vector.tensor_copy)
-        quantise_z(2)
-        weave_cells(0, 4, nc.vector.tensor_copy)
-        quantise_z(3)
-        quantise_z(4)
-
+        weave_cells(7, nc.scalar.copy)
+        weave_cells(0, nc.vector.tensor_copy)
         out_rows = out.rearrange("(m p) v -> p m v", p=P)
-        for c, (a, b) in enumerate(chunks):
-            n = b - a
-            res = held.tile([P, 2, n], F32, name=f"res{c}")
-            for m in range(2):
-                bank = psum.tile([P, 512], F32, name="bank")
-                nc.tensor.matmul_mx(
-                    out=bank[:, 0:n],
-                    lhsT=w2q[:, m * P : (m + 1) * P].bitcast(FP8X4),
-                    lhsT_scale=w2s[:, m * P : (m + 1) * P],
-                    rhs=zq[:, a:b].bitcast(FP8X4),
-                    rhs_scale=zs[:, a:b],
-                    start=True,
-                    stop=True,
+        stores = ((0, 1), (1, 3), (3, 5), (5, 6), (6, 7), (7, 8))
+        for first, last in stores:
+            res = held.tile([P, 2, 128 * (last - first)], F32, name=f"res{first}")
+            for c in range(first, last):
+                if c < 6:
+                    weave_cells(c + 1, nc.vector.tensor_copy)
+                cols = slice(128 * c, 128 * (c + 1))
+                nc.vector.quantize_mx(
+                    out=zq[:, cols].bitcast(FP8X4), scales=zs[:, cols], in_=woven[c][:].rearrange("p v j -> p (v j)")
                 )
-                copy = nc.vector.tensor_copy if c >= 3 and m == 1 else nc.scalar.copy
-                copy(out=res[:, m, :], in_=bank[:, 0:n])
-                if n == 256:
-                    nc.sync.dma_start(out=out_rows[:, m, a:b], in_=res[:, m, :])
-            if n == 128:
-                nc.sync.dma_start(out=out_rows[:, :, a:b], in_=res[:])
+                bank = psum.tile([P, 4, 128], F32, name="bank")
+                for m in range(2):
+                    nc.tensor.matmul_mx(
+                        out=bank[:, m, :],
+                        lhsT=w2q[:, m * P : (m + 1) * P].bitcast(FP8X4),
+                        lhsT_scale=w2s[:, m * P : (m + 1) * P],
+                        rhs=zq[:, cols].bitcast(FP8X4),
+                        rhs_scale=zs[:, cols],
+                        start=True,
+                        stop=True,
+                    )
+                copy = nc.vector.tensor_copy if c == 7 else nc.scalar.copy
+                copy(out=res[:, :, 128 * (c - first) : 128 * (c - first + 1)], in_=bank[:, 0:2, :])
+            nc.sync.dma_start(out=out_rows[:, :, 128 * first : 128 * last], in_=res[:])

@@ -77,12 +77,12 @@ def tile_picked_voxel_silu_e_kernel(tc, xT, w1, w2, gate, offs, pos1, out):
         grouped = [held.tile([P, 128, 4], BF16, name=f"w1_grouped{t}", align_bytes=64) for t in range(4)]
         for u in range(2):
             w1_from = w1_raw[u][:].rearrange("p e (g t i) -> p t g i e", t=4, i=8)
-            for t, copy in ((1, nc.vector.tensor_copy), (3, nc.scalar.copy), (0, nc.vector.tensor_copy), (2, nc.scalar.copy)):
+            for t, copy in ((0, nc.vector.tensor_copy), (3, nc.scalar.copy), (1, nc.vector.tensor_copy), (2, nc.scalar.copy)):
                 copy(
                     out=grouped[t][:].rearrange("p (g i) j -> p g i j", i=8)[:, :, :, 2 * u : 2 * u + 2],
                     in_=w1_from[:, t],
                 )
-        for t in (1, 0, 3, 2):
+        for t in (0, 1, 3, 2):
             nc.vector.quantize_mx(
                 out=w1q[:, t, :].bitcast(FP8X4), scales=w1s[:, t, :], in_=grouped[t][:].rearrange("p m j -> p (m j)")
             )
@@ -107,7 +107,7 @@ def tile_picked_voxel_silu_e_kernel(tc, xT, w1, w2, gate, offs, pos1, out):
             return z[t][:].indirect(pos_sb[:, a // 16 : b // 16])
 
         h = [held.tile([P, S], F32, name=f"h{t}", tag=f"h{t}", align_bytes=64) for t in range(4)]
-        gated = {t: held.tile([P, S], F32, name=f"gated{t}") for t in (1, 3)}
+        gated = {t: held.tile([P, S], F32, name=f"gated{t}", tag=f"gated{t}", align_bytes=64) for t in (1, 3)}
 
         def plane_layer(t, edges):
             first_layer(h[t][:, edges[0] : edges[-1]], [(t, a, b) for a, b in zip(edges, edges[1:])])
@@ -129,75 +129,89 @@ def tile_picked_voxel_silu_e_kernel(tc, xT, w1, w2, gate, offs, pos1, out):
                 if start <= a < stop:
                     return tile[:].rearrange("p (t v) -> p t v", t=4)[:, :, a - start : b - start]
 
-        plane_layer(1, (0, HALF))
         plane_layer(0, (0, 128))
+        plane_layer(1, (0, HALF))
         plane_layer(1, (HALF, S))
         plane_layer(0, (128, 256, S))
-        weigh(1, 0, HALF)
+        plane_layer(3, (0, S))
         scatter_on_vector(0, 0, 128)
+        weigh(1, 0, HALF)
         weigh(1, HALF, S)
         scatter_on_vector(0, 128, S)
         for a, b in parts:
             nc.sync.dma_start(out=plane_cells(a, b)[:, 0, :], in_=z[0][:, a:b])
         scatter_on_scalar(1, 0, HALF)
-        plane_layer(3, (0, S))
         plane_layer(2, (0, S))
         scatter_on_scalar(1, HALF, S)
         for a, b in parts:
             nc.sync.dma_start(out=plane_cells(a, b)[:, 1, :], in_=z[1][:, a:b])
-        weigh(3, 0, S)
+        weigh(3, 128, S)
+        scatter_on_vector(3, 0, 128)
         scatter_on_vector(2, 0, S)
-        w2_grouped = held.tile([P, N, 4], BF16, name="w2_grouped", tag="h3", align_bytes=64)
+        scatter_on_scalar(3, 128, S)
         w2_from = w2_raw[:].rearrange("p j m -> p m j")
-        scatter_on_scalar(3, 0, HALF)
-        nc.scalar.copy(out=w2_grouped[:, 0:64, :], in_=w2_from[:, 0:64, :])
-        scatter_on_scalar(3, HALF, S)
-        nc.vector.tensor_copy(out=w2_grouped[:, 64:N, :], in_=w2_from[:, 64:N, :])
+        w2_grouped = []
+        for m, (copy, tag) in enumerate(((nc.scalar.copy, "h3"), (nc.vector.tensor_copy, "gated3"))):
+            tile = held.tile([P, P, 4], BF16, name=f"w2_grouped{m}", tag=tag, align_bytes=64)
+            copy(out=tile[:], in_=w2_from[:, m * P : (m + 1) * P, :])
+            w2_grouped.append(tile)
         nc.vector.tensor_copy(out=plane_cells(*parts[0])[:, 2, :], in_=z[2][:, 0:HALF])
         w2q = held.tile([P, N], U32, name="w2q", align_bytes=64)
         w2s = held.tile([P, N], U8, name="w2s", align_bytes=64)
-        nc.vector.quantize_mx(
-            out=w2q[:].bitcast(FP8X4), scales=w2s[:], in_=w2_grouped[:].rearrange("p m j -> p (m j)")
-        )
+        for m in (1, 0):
+            nc.vector.quantize_mx(
+                out=w2q[:, m * P : (m + 1) * P].bitcast(FP8X4),
+                scales=w2s[:, m * P : (m + 1) * P],
+                in_=w2_grouped[m][:].rearrange("p m j -> p (m j)"),
+            )
+        for t, a, b in ((3, 0, HALF), (3, HALF, 512), (2, HALF, 768), (3, 512, 768)):
+            nc.scalar.copy(out=plane_cells(a, b)[:, t, :], in_=z[t][:, a:b])
+        for t, a in ((3, 768), (2, 768)):
+            nc.sync.dma_start(out=plane_cells(a, V)[:, t, :], in_=z[t][:, a:V])
 
-        nc.vector.tensor_copy(out=plane_cells(*parts[1])[:, 2, :], in_=z[2][:, HALF:V])
-        for a, b in ((0, 128), (128, HALF), (HALF, 512), (512, V)):
-            nc.scalar.copy(out=plane_cells(a, b)[:, 3, :], in_=z[3][:, a:b])
-
-        woven = [held.tile([P, 128, 4], BF16, name=f"woven{c}", align_bytes=64) for c in range(8)]
+        woven = held.tile([P, 4 * V], BF16, name="woven", align_bytes=64)
         zs = held.tile([P, V], U8, name="zs", align_bytes=64)
         zq = held.tile([P, V], U32, name="zq", align_bytes=64)
+        out_rows = out.rearrange("(m p) v -> p m v", p=P)
 
-        def weave_cells(c, copy):
+        def weave_cells(a, b, copy):
             copy(
-                out=woven[c][:].rearrange("p (w i) t -> p w t i", i=4),
-                in_=plane_cells(128 * c, 128 * (c + 1)).rearrange("p t (w i) -> p w t i", i=4),
+                out=woven[:, 4 * a : 4 * b].rearrange("p (w i t) -> p w t i", i=4, t=4),
+                in_=plane_cells(a, b).rearrange("p t (w i) -> p w t i", i=4),
             )
 
-        weave_cells(7, nc.scalar.copy)
-        weave_cells(0, nc.vector.tensor_copy)
-        out_rows = out.rearrange("(m p) v -> p m v", p=P)
-        stores = ((0, 1), (1, 3), (3, 5), (5, 6), (6, 7), (7, 8))
-        for first, last in stores:
-            res = held.tile([P, 2, 128 * (last - first)], F32, name=f"res{first}")
-            for c in range(first, last):
-                if c < 6:
-                    weave_cells(c + 1, nc.vector.tensor_copy)
-                cols = slice(128 * c, 128 * (c + 1))
-                nc.vector.quantize_mx(
-                    out=zq[:, cols].bitcast(FP8X4), scales=zs[:, cols], in_=woven[c][:].rearrange("p v j -> p (v j)")
-                )
-                bank = psum.tile([P, 4, 128], F32, name="bank")
-                for m in range(2):
-                    nc.tensor.matmul_mx(
-                        out=bank[:, m, :],
-                        lhsT=w2q[:, m * P : (m + 1) * P].bitcast(FP8X4),
-                        lhsT_scale=w2s[:, m * P : (m + 1) * P],
-                        rhs=zq[:, cols].bitcast(FP8X4),
-                        rhs_scale=zs[:, cols],
-                        start=True,
-                        stop=True,
-                    )
-                copy = nc.vector.tensor_copy if c == 7 else nc.scalar.copy
-                copy(out=res[:, :, 128 * (c - first) : 128 * (c - first + 1)], in_=bank[:, 0:2, :])
-            nc.sync.dma_start(out=out_rows[:, :, 128 * first : 128 * last], in_=res[:])
+        def second_layer(dst, m, a, b):
+            nc.tensor.matmul_mx(
+                out=dst,
+                lhsT=w2q[:, m * P : (m + 1) * P].bitcast(FP8X4),
+                lhsT_scale=w2s[:, m * P : (m + 1) * P],
+                rhs=zq[:, a:b].bitcast(FP8X4),
+                rhs_scale=zs[:, a:b],
+                start=True,
+                stop=True,
+            )
+
+        def finish(a, b, copy):
+            nc.vector.quantize_mx(out=zq[:, a:b].bitcast(FP8X4), scales=zs[:, a:b], in_=woven[:, 4 * a : 4 * b])
+            for ms in (((0, 1),) if b - a == 128 else ((0,), (1,))):
+                bank = psum.tile([P, 512], F32, name="bank")
+                sums = bank[:, 0:HALF].rearrange("p (m v) -> p m v", m=len(ms))
+                for m in ms:
+                    second_layer(sums[:, m - ms[0], :], m, a, b)
+                res = held.tile([P, len(ms), b - a], F32, name=f"res{a}_{ms[0]}")
+                copy(out=res[:], in_=sums)
+                nc.sync.dma_start(out=out_rows[:, ms[0] : ms[-1] + 1, a:b], in_=res[:])
+
+        weave_cells(384, 512, nc.scalar.copy)
+        weave_cells(0, 128, nc.vector.tensor_copy)
+        weave_cells(128, 256, nc.vector.tensor_copy)
+        finish(0, 128, nc.scalar.copy)
+        weave_cells(256, 384, nc.vector.tensor_copy)
+        finish(128, 256, nc.scalar.copy)
+        weave_cells(512, 768, nc.vector.tensor_copy)
+        finish(256, 512, nc.scalar.copy)
+        finish(512, 768, nc.scalar.copy)
+        weave_cells(768, 896, nc.vector.tensor_copy)
+        weave_cells(896, V, nc.vector.tensor_copy)
+        finish(768, 896, nc.scalar.copy)
+        finish(896, V, nc.vector.tensor_copy)

@@ -149,21 +149,17 @@ def tile_picked_voxel_silu_e_kernel(tc, xT, w1, w2, gate, offs, pos1, out):
         scatter_on_vector(3, 0, 128)
         scatter_on_vector(2, 0, S)
         scatter_on_scalar(3, 128, S)
-        w2_from = w2_raw[:].rearrange("p j m -> p m j")
-        w2_grouped = []
-        for m, (copy, tag) in enumerate(((nc.scalar.copy, "h3"), (nc.vector.tensor_copy, "gated3"))):
-            tile = held.tile([P, P, 4], BF16, name=f"w2_grouped{m}", tag=tag, align_bytes=64)
-            copy(out=tile[:], in_=w2_from[:, m * P : (m + 1) * P, :])
-            w2_grouped.append(tile)
+        w2_grouped = held.tile([P, N, 4], BF16, name="w2_grouped", tag="gated3", align_bytes=64)
+        nc.vector.tensor_copy(
+            out=w2_grouped[:].rearrange("p (w i) t -> p w t i", i=4),
+            in_=w2_raw[:].rearrange("p t (w i) -> p w t i", i=4),
+        )
         nc.vector.tensor_copy(out=plane_cells(*parts[0])[:, 2, :], in_=z[2][:, 0:HALF])
         w2q = held.tile([P, N], U32, name="w2q", align_bytes=64)
         w2s = held.tile([P, N], U8, name="w2s", align_bytes=64)
-        for m in (1, 0):
-            nc.vector.quantize_mx(
-                out=w2q[:, m * P : (m + 1) * P].bitcast(FP8X4),
-                scales=w2s[:, m * P : (m + 1) * P],
-                in_=w2_grouped[m][:].rearrange("p m j -> p (m j)"),
-            )
+        nc.vector.quantize_mx(
+            out=w2q[:].bitcast(FP8X4), scales=w2s[:], in_=w2_grouped[:].rearrange("p m j -> p (m j)")
+        )
         for t, a, b in ((3, 0, HALF), (3, HALF, 512), (2, HALF, 768), (3, 512, 768)):
             nc.scalar.copy(out=plane_cells(a, b)[:, t, :], in_=z[t][:, a:b])
         for t, a in ((3, 768), (2, 768)):

@@ -121,7 +121,7 @@ def tile_picked_voxel_silu_e_kernel(tc, xT, w1, w2, gate, offs, pos1, out):
         def scatter_on_scalar(t, a, b):
             nc.scalar.activation(cells(t, a, b), gated[t][:, a:b], COPY)
 
-        parts = ((0, HALF), (HALF, V))
+        parts = tuple((a, a + HALF) for a in range(0, V, HALF))
         planes = [held.tile([P, 4 * (b - a)], F32, name=f"planes{a}") for a, b in parts]
 
         def plane_cells(a, b):
@@ -151,16 +151,15 @@ def tile_picked_voxel_silu_e_kernel(tc, xT, w1, w2, gate, offs, pos1, out):
         scatter_on_scalar(3, 128, S)
         w2_grouped = held.tile([P, N, 4], BF16, name="w2_grouped", tag="gated3", align_bytes=64)
         nc.vector.tensor_copy(
-            out=w2_grouped[:].rearrange("p (w i) t -> p w t i", i=4),
-            in_=w2_raw[:].rearrange("p t (w i) -> p w t i", i=4),
+            out=w2_grouped[:].rearrange("p (w i) t -> p w t i", i=2),
+            in_=w2_raw[:].rearrange("p t (w i) -> p w t i", i=2),
         )
-        nc.vector.tensor_copy(out=plane_cells(*parts[0])[:, 2, :], in_=z[2][:, 0:HALF])
         w2q = held.tile([P, N], U32, name="w2q", align_bytes=64)
         w2s = held.tile([P, N], U8, name="w2s", align_bytes=64)
         nc.vector.quantize_mx(
             out=w2q[:].bitcast(FP8X4), scales=w2s[:], in_=w2_grouped[:].rearrange("p m j -> p (m j)")
         )
-        for t, a, b in ((3, 0, HALF), (3, HALF, 512), (2, HALF, 768), (3, 512, 768)):
+        for t, a, b in ((3, 0, HALF), (3, HALF, 512), (2, 0, HALF), (2, HALF, 512), (3, 512, 768), (2, 512, 768)):
             nc.scalar.copy(out=plane_cells(a, b)[:, t, :], in_=z[t][:, a:b])
         for t, a in ((3, 768), (2, 768)):
             nc.sync.dma_start(out=plane_cells(a, V)[:, t, :], in_=z[t][:, a:V])
@@ -172,8 +171,8 @@ def tile_picked_voxel_silu_e_kernel(tc, xT, w1, w2, gate, offs, pos1, out):
 
         def weave_cells(a, b, copy):
             copy(
-                out=woven[:, 4 * a : 4 * b].rearrange("p (w i t) -> p w t i", i=4, t=4),
-                in_=plane_cells(a, b).rearrange("p t (w i) -> p w t i", i=4),
+                out=woven[:, 4 * a : 4 * b].rearrange("p (w i t) -> p w t i", i=2, t=4),
+                in_=plane_cells(a, b).rearrange("p t (w i) -> p w t i", i=2),
             )
 
         def second_layer(dst, m, a, b):

@@ -106,17 +106,22 @@ def tile_picked_voxel_silu_e_kernel(tc, xT, w1, w2, gate, offs, pos1, out):
         def cells(t, a, b):
             return z[t][:].indirect(pos_sb[:, a // 16 : b // 16])
 
-        h = [held.tile([P, S], F32, name=f"h{t}", tag=f"h{t}", align_bytes=64) for t in range(4)]
-        gated = {t: held.tile([P, S], F32, name=f"gated{t}", tag=f"gated{t}", align_bytes=64) for t in (1, 3)}
+        h = {}
+        gated = {t: held.tile([P, HALF], F32, name=f"gated{t}") for t in (0, 1, 3)}
 
-        def plane_layer(t, edges):
-            first_layer(h[t][:, edges[0] : edges[-1]], [(t, a, b) for a, b in zip(edges, edges[1:])])
+        def silu_of(*pieces):
+            tile = held.tile([P, sum(b - a for t, a, b in pieces)], F32, name=f"h{len(h)}", tag=f"h{len(h)}", align_bytes=64)
+            first_layer(tile[:], pieces)
+            at = 0
+            for t, a, b in pieces:
+                h[t, a] = tile[:, at : at + b - a]
+                at = at + b - a
 
-        def weigh(t, a, b):
-            nc.vector.tensor_tensor(gated[t][:, a:b], h[t][:, a:b], gate_sb[:, a:b], MULT)
+        def weigh(engine, t, a, b, start):
+            engine.tensor_tensor(gated[t][:, a:b], h[t, start][:, a - start : b - start], gate_sb[:, a:b], MULT)
 
         def scatter_on_vector(t, a, b):
-            nc.vector.tensor_tensor(cells(t, a, b), h[t][:, a:b], gate_sb[:, a:b], MULT)
+            nc.vector.tensor_copy(cells(t, a, b), gated[t][:, a:b])
 
         def scatter_on_scalar(t, a, b):
             nc.scalar.activation(cells(t, a, b), gated[t][:, a:b], COPY)
@@ -129,27 +134,32 @@ def tile_picked_voxel_silu_e_kernel(tc, xT, w1, w2, gate, offs, pos1, out):
                 if start <= a < stop:
                     return tile[:].rearrange("p (t v) -> p t v", t=4)[:, :, a - start : b - start]
 
-        plane_layer(0, (0, 128))
-        plane_layer(1, (0, HALF))
-        plane_layer(1, (HALF, S))
-        plane_layer(0, (128, 256, S))
-        plane_layer(3, (0, S))
-        scatter_on_vector(0, 0, 128)
-        weigh(1, 0, HALF)
-        weigh(1, HALF, S)
-        scatter_on_vector(0, 128, S)
+        silu_of((0, 0, 128))
+        silu_of((0, 128, HALF), (1, 0, HALF))
+        silu_of((3, 0, HALF), (0, HALF, S))
+        silu_of((1, HALF, S), (3, HALF, S))
+        nc.vector.tensor_tensor(cells(0, 0, 128), h[0, 0], gate_sb[:, 0:128], MULT)
+        weigh(nc.vector, 1, 0, HALF, 0)
+        weigh(nc.vector, 0, 128, HALF, 128)
+        weigh(nc.vector, 3, 0, 128, 0)
+        scatter_on_vector(0, 128, HALF)
+        late = held.tile([P, 896], F32, name="gated_late", tag="h1", align_bytes=64)
+        at = 0
+        for t, start, a, b in ((0, HALF, HALF, S), (1, HALF, HALF, S), (3, 0, 128, HALF), (3, HALF, HALF, S)):
+            nc.gpsimd.tensor_tensor(late[:, at : at + b - a], h[t, start][:, a - start : b - start], gate_sb[:, a:b], MULT)
+            at = at + b - a
+        scatter_on_vector(3, 0, 128)
+        nc.vector.tensor_copy(cells(0, HALF, S), late[:, 0:HALF])
         for a, b in parts:
             nc.sync.dma_start(out=plane_cells(a, b)[:, 0, :], in_=z[0][:, a:b])
         scatter_on_scalar(1, 0, HALF)
-        plane_layer(2, (0, S))
-        scatter_on_scalar(1, HALF, S)
+        silu_of((2, 0, S))
+        nc.scalar.activation(cells(1, HALF, S), late[:, HALF:S], COPY)
         for a, b in parts:
             nc.sync.dma_start(out=plane_cells(a, b)[:, 1, :], in_=z[1][:, a:b])
-        weigh(3, 128, S)
-        scatter_on_vector(3, 0, 128)
-        scatter_on_vector(2, 0, S)
-        scatter_on_scalar(3, 128, S)
-        w2_grouped = held.tile([P, N, 4], BF16, name="w2_grouped", tag="gated3", align_bytes=64)
+        nc.vector.tensor_tensor(cells(2, 0, S), h[2, 0], gate_sb[:], MULT)
+        nc.scalar.activation(cells(3, 128, S), late[:, S:896], COPY)
+        w2_grouped = held.tile([P, N, 4], BF16, name="w2_grouped", tag="h1", align_bytes=64)
         nc.vector.tensor_copy(
             out=w2_grouped[:].rearrange("p (w i) t -> p w t i", i=2),
             in_=w2_raw[:].rearrange("p t (w i) -> p w t i", i=2),
@@ -159,7 +169,7 @@ def tile_picked_voxel_silu_e_kernel(tc, xT, w1, w2, gate, offs, pos1, out):
         nc.vector.quantize_mx(
             out=w2q[:].bitcast(FP8X4), scales=w2s[:], in_=w2_grouped[:].rearrange("p m j -> p (m j)")
         )
-        for t, a, b in ((3, 0, HALF), (3, HALF, 512), (2, 0, HALF), (2, HALF, 512), (3, 512, 768), (2, 512, 768)):
+        for t, a, b in ((3, 0, HALF), (2, 0, HALF), (3, HALF, 512), (2, HALF, 512), (3, 512, 768), (2, 512, 768)):
             nc.scalar.copy(out=plane_cells(a, b)[:, t, :], in_=z[t][:, a:b])
         for t, a in ((3, 768), (2, 768)):
             nc.sync.dma_start(out=plane_cells(a, V)[:, t, :], in_=z[t][:, a:V])

@@ -17,6 +17,7 @@ MULT = mybir.AluOpType.mult
 
 P = 128
 HALF = 256
+SHARE = 128
 
 
 def tile_picked_voxel_silu_e_kernel(tc, xT, w1, w2, gate, offs, pos1, out):
@@ -141,35 +142,40 @@ def tile_picked_voxel_silu_e_kernel(tc, xT, w1, w2, gate, offs, pos1, out):
         nc.vector.tensor_tensor(cells(0, 0, 128), h[0, 0], gate_sb[:, 0:128], MULT)
         weigh(nc.vector, 1, 0, HALF, 0)
         weigh(nc.vector, 0, 128, HALF, 128)
-        weigh(nc.vector, 3, 0, 128, 0)
+        weigh(nc.vector, 3, 0, SHARE, 0)
         scatter_on_vector(0, 128, HALF)
-        late = held.tile([P, 896], F32, name="gated_late", tag="h1", align_bytes=64)
-        at = 0
-        for t, start, a, b in ((0, HALF, HALF, S), (1, HALF, HALF, S), (3, 0, 128, HALF), (3, HALF, HALF, S)):
-            nc.gpsimd.tensor_tensor(late[:, at : at + b - a], h[t, start][:, a - start : b - start], gate_sb[:, a:b], MULT)
-            at = at + b - a
-        scatter_on_vector(3, 0, 128)
+        late = held.tile([P, HALF + S - SHARE], F32, name="gated_late", tag="h1", align_bytes=64)
+        late_1 = held.tile([P, HALF], F32, name="gated_late_1", tag="late_1", align_bytes=64)
+        for dst, t, start, a, b in (
+            (late[:, 0:HALF], 0, HALF, HALF, S),
+            (late_1[:], 1, HALF, HALF, S),
+            (late[:, HALF : S - SHARE], 3, 0, SHARE, HALF),
+            (late[:, S - SHARE : HALF + S - SHARE], 3, HALF, HALF, S),
+        ):
+            nc.gpsimd.tensor_tensor(dst, h[t, start][:, a - start : b - start], gate_sb[:, a:b], MULT)
+        scatter_on_vector(3, 0, SHARE)
         nc.vector.tensor_copy(cells(0, HALF, S), late[:, 0:HALF])
         for a, b in parts:
             nc.sync.dma_start(out=plane_cells(a, b)[:, 0, :], in_=z[0][:, a:b])
         scatter_on_scalar(1, 0, HALF)
         silu_of((2, 0, S))
-        nc.scalar.activation(cells(1, HALF, S), late[:, HALF:S], COPY)
+        nc.scalar.activation(cells(1, HALF, S), late_1[:], COPY)
         for a, b in parts:
             nc.sync.dma_start(out=plane_cells(a, b)[:, 1, :], in_=z[1][:, a:b])
         nc.vector.tensor_tensor(cells(2, 0, S), h[2, 0], gate_sb[:], MULT)
-        nc.scalar.activation(cells(3, 128, S), late[:, S:896], COPY)
-        w2_grouped = held.tile([P, N, 4], BF16, name="w2_grouped", tag="h1", align_bytes=64)
+        nc.scalar.activation(cells(3, SHARE, S), late[:, HALF : HALF + S - SHARE], COPY)
+        w2_grouped = held.tile([P, N, 4], BF16, name="w2_grouped", tag="late_1", align_bytes=64)
         nc.vector.tensor_copy(
             out=w2_grouped[:].rearrange("p (w i) t -> p w t i", i=2),
             in_=w2_raw[:].rearrange("p t (w i) -> p w t i", i=2),
         )
+        nc.vector.tensor_copy(out=plane_cells(0, HALF)[:, 2, :], in_=z[2][:, 0:HALF])
         w2q = held.tile([P, N], U32, name="w2q", align_bytes=64)
         w2s = held.tile([P, N], U8, name="w2s", align_bytes=64)
         nc.vector.quantize_mx(
             out=w2q[:].bitcast(FP8X4), scales=w2s[:], in_=w2_grouped[:].rearrange("p m j -> p (m j)")
         )
-        for t, a, b in ((3, 0, HALF), (2, 0, HALF), (3, HALF, 512), (2, HALF, 512), (3, 512, 768), (2, 512, 768)):
+        for t, a, b in ((3, 0, HALF), (3, HALF, 512), (2, HALF, 512), (3, 512, 768), (2, 512, 768)):
             nc.scalar.copy(out=plane_cells(a, b)[:, t, :], in_=z[t][:, a:b])
         for t, a in ((3, 768), (2, 768)):
             nc.sync.dma_start(out=plane_cells(a, V)[:, t, :], in_=z[t][:, a:V])
@@ -207,11 +213,11 @@ def tile_picked_voxel_silu_e_kernel(tc, xT, w1, w2, gate, offs, pos1, out):
                 copy(out=res[:], in_=sums)
                 nc.sync.dma_start(out=out_rows[:, ms[0] : ms[-1] + 1, a:b], in_=res[:])
 
-        weave_cells(384, 512, nc.scalar.copy)
+        weave_cells(320, 512, nc.scalar.copy)
         weave_cells(0, 128, nc.vector.tensor_copy)
         weave_cells(128, 256, nc.vector.tensor_copy)
         finish(0, 128, nc.scalar.copy)
-        weave_cells(256, 384, nc.vector.tensor_copy)
+        weave_cells(256, 320, nc.vector.tensor_copy)
         finish(128, 256, nc.scalar.copy)
         weave_cells(512, 768, nc.vector.tensor_copy)
         finish(256, 512, nc.scalar.copy)

@@ -34,20 +34,20 @@ def tile_picked_voxel_silu_e_kernel(tc, xT, w1, w2, gate, offs, pos1, out):
         pos_sb = held.tile([P, S // 16], U16, name="pos_sb")
         x_raw = []
         for j in range(4):
-            t = held.tile([P, T], F32, name=f"x_raw{j}")
+            t = held.tile([P, T], F32, name=f"x_raw{j}", align_bytes=256)
             nc.sync.dma_start(out=t[:], in_=x_rows[:, j, :])
             x_raw.append(t)
             if j == 0:
                 nc.sync.dma_start(offs_sb[:], offs)
         w1_raw = []
         for u in range(2):
-            t = held.tile([P, 2, H], F32, name=f"w1_raw{u}")
+            t = held.tile([P, 2, H], F32, name=f"w1_raw{u}", align_bytes=256)
             nc.sync.dma_start(out=t[:], in_=w1_rows[:, 2 * u : 2 * u + 2, :])
             w1_raw.append(t)
         nc.sync.dma_start(pos_sb[:], pos1)
-        gate_sb = held.tile([P, S], F32, name="gate_sb")
+        gate_sb = held.tile([P, S], F32, name="gate_sb", align_bytes=256)
         nc.sync.dma_start(out=gate_sb[:], in_=gate)
-        w2_raw = held.tile([P, 4, N], F32, name="w2_raw")
+        w2_raw = held.tile([P, 4, N], F32, name="w2_raw", align_bytes=256)
         for t in range(4):
             nc.sync.dma_start(out=w2_raw[:, t, :], in_=w2_rows[t])
 
@@ -56,7 +56,7 @@ def tile_picked_voxel_silu_e_kernel(tc, xT, w1, w2, gate, offs, pos1, out):
         nc.vector.memset(warm[:], 0.0)
         nc.scalar.activation(warm_out[:], warm[:], SILU)
 
-        z = [held.tile([P, V], F32, name=f"z{t}") for t in range(4)]
+        z = [held.tile([P, V], F32, name=f"z{t}", align_bytes=256) for t in range(4)]
         for t in range(4):
             nc.vector.memset(z[t][:], 0.0)
 
@@ -128,7 +128,7 @@ def tile_picked_voxel_silu_e_kernel(tc, xT, w1, w2, gate, offs, pos1, out):
             nc.scalar.activation(cells(t, a, b), gated[t][:, a:b], COPY)
 
         parts = tuple((a, a + HALF) for a in range(0, V, HALF))
-        planes = [held.tile([P, 4 * (b - a)], F32, name=f"planes{a}") for a, b in parts]
+        planes = [held.tile([P, 4 * (b - a)], F32, name=f"planes{a}", align_bytes=256) for a, b in parts]
 
         def plane_cells(a, b):
             for (start, stop), tile in zip(parts, planes):
@@ -175,7 +175,7 @@ def tile_picked_voxel_silu_e_kernel(tc, xT, w1, w2, gate, offs, pos1, out):
         nc.vector.quantize_mx(
             out=w2q[:].bitcast(FP8X4), scales=w2s[:], in_=w2_grouped[:].rearrange("p m j -> p (m j)")
         )
-        for t, a, b in ((3, 0, HALF), (3, HALF, 512), (2, HALF, 512), (3, 512, 768), (2, 512, 768)):
+        for t, a, b in ((3, 0, HALF), (3, HALF, 512), (2, HALF, 512), (3, 512, 768)):
             nc.scalar.copy(out=plane_cells(a, b)[:, t, :], in_=z[t][:, a:b])
         for t, a in ((3, 768), (2, 768)):
             nc.sync.dma_start(out=plane_cells(a, V)[:, t, :], in_=z[t][:, a:V])
@@ -202,27 +202,30 @@ def tile_picked_voxel_silu_e_kernel(tc, xT, w1, w2, gate, offs, pos1, out):
                 stop=True,
             )
 
-        def finish(a, b, copy):
+        def finish(a, b, copies):
             nc.vector.quantize_mx(out=zq[:, a:b].bitcast(FP8X4), scales=zs[:, a:b], in_=woven[:, 4 * a : 4 * b])
-            for ms in (((0, 1),) if b - a == 128 else ((0,), (1,))):
+            res = held.tile([P, 2, b - a], F32, name=f"res{a}", align_bytes=256)
+            for ms, copy in zip(((0, 1),) if len(copies) == 1 else ((0,), (1,)), copies):
                 bank = psum.tile([P, 512], F32, name="bank")
-                sums = bank[:, 0:HALF].rearrange("p (m v) -> p m v", m=len(ms))
+                sums = bank[:, 0 : len(ms) * (b - a)].rearrange("p (m v) -> p m v", m=len(ms))
                 for m in ms:
                     second_layer(sums[:, m - ms[0], :], m, a, b)
-                res = held.tile([P, len(ms), b - a], F32, name=f"res{a}_{ms[0]}")
-                copy(out=res[:], in_=sums)
-                nc.sync.dma_start(out=out_rows[:, ms[0] : ms[-1] + 1, a:b], in_=res[:])
+                copy(out=res[:, ms[0] : ms[-1] + 1, :], in_=sums)
+                if b - a == HALF:
+                    nc.sync.dma_start(out=out_rows[:, ms[0], a:b], in_=res[:, ms[0], :])
+            if b - a == 128:
+                nc.sync.dma_start(out=out_rows[:, :, a:b], in_=res[:])
 
-        weave_cells(320, 512, nc.scalar.copy)
+        weave_cells(256, 512, nc.scalar.copy)
         weave_cells(0, 128, nc.vector.tensor_copy)
+        nc.vector.tensor_copy(out=plane_cells(512, 768)[:, 2, :], in_=z[2][:, 512:768])
         weave_cells(128, 256, nc.vector.tensor_copy)
-        finish(0, 128, nc.scalar.copy)
-        weave_cells(256, 320, nc.vector.tensor_copy)
-        finish(128, 256, nc.scalar.copy)
+        finish(0, 128, [nc.scalar.copy])
         weave_cells(512, 768, nc.vector.tensor_copy)
-        finish(256, 512, nc.scalar.copy)
-        finish(512, 768, nc.scalar.copy)
+        finish(128, 256, [nc.scalar.copy])
+        finish(256, 512, [nc.scalar.copy] * 2)
+        finish(512, 768, [nc.scalar.copy] * 2)
         weave_cells(768, 896, nc.vector.tensor_copy)
         weave_cells(896, V, nc.vector.tensor_copy)
-        finish(768, 896, nc.scalar.copy)
-        finish(896, V, nc.vector.tensor_copy)
+        finish(768, 896, [nc.vector.tensor_copy])
+        finish(896, V, [nc.scalar.copy, nc.vector.tensor_copy])

@@ -14,6 +14,7 @@ FP8X4 = mybir.dt.float8_e4m3fn_x4
 SILU = mybir.ActivationFunctionType.Silu
 COPY = mybir.ActivationFunctionType.Copy
 MULT = mybir.AluOpType.mult
+ADD = mybir.AluOpType.add
 
 P = 128
 HALF = 256
@@ -137,45 +138,42 @@ def tile_picked_voxel_silu_e_kernel(tc, xT, w1, w2, gate, offs, pos1, out):
 
         silu_of((0, 0, 128))
         silu_of((0, 128, HALF), (1, 0, HALF))
-        silu_of((3, 0, HALF), (0, HALF, S))
-        silu_of((1, HALF, S), (3, HALF, S))
+        silu_of((3, 0, SHARE), (0, HALF, S))
+        silu_of((1, HALF, S))
+        silu_of((2, 0, S))
         nc.vector.tensor_tensor(cells(0, 0, 128), h[0, 0], gate_sb[:, 0:128], MULT)
         weigh(nc.vector, 1, 0, HALF, 0)
         weigh(nc.vector, 0, 128, HALF, 128)
         weigh(nc.vector, 3, 0, SHARE, 0)
         scatter_on_vector(0, 128, HALF)
-        late = held.tile([P, HALF + S - SHARE], F32, name="gated_late", tag="h1", align_bytes=64)
-        late_1 = held.tile([P, HALF], F32, name="gated_late_1", tag="late_1", align_bytes=64)
-        for dst, t, start, a, b in (
-            (late[:, 0:HALF], 0, HALF, HALF, S),
-            (late_1[:], 1, HALF, HALF, S),
-            (late[:, HALF : S - SHARE], 3, 0, SHARE, HALF),
-            (late[:, S - SHARE : HALF + S - SHARE], 3, HALF, HALF, S),
-        ):
-            nc.gpsimd.tensor_tensor(dst, h[t, start][:, a - start : b - start], gate_sb[:, a:b], MULT)
+        late = {}
+        for t, a, tag in ((0, HALF, "h1"), (1, HALF, "late1"), (2, 0, "late2")):
+            late[t] = held.tile([P, S - a], F32, name=f"late{t}", tag=tag, align_bytes=64)
+            nc.gpsimd.tensor_tensor(late[t][:], h[t, a], gate_sb[:, a:S], MULT)
         scatter_on_vector(3, 0, SHARE)
-        nc.vector.tensor_copy(cells(0, HALF, S), late[:, 0:HALF])
+        nc.vector.tensor_copy(cells(0, HALF, S), late[0][:])
         for a, b in parts:
             nc.sync.dma_start(out=plane_cells(a, b)[:, 0, :], in_=z[0][:, a:b])
         scatter_on_scalar(1, 0, HALF)
-        silu_of((2, 0, S))
-        nc.scalar.activation(cells(1, HALF, S), late_1[:], COPY)
+        late[3] = held.tile([P, S - SHARE], F32, name="late3")
+        rest = held.tile([P, S - SHARE], F32, name="h_rest", tag="h_rest", align_bytes=64)
+        first_layer(rest[:], ((3, SHARE, HALF), (3, HALF, S)))
+        nc.scalar.activation(cells(1, HALF, S), late[1][:], COPY)
         for a, b in parts:
             nc.sync.dma_start(out=plane_cells(a, b)[:, 1, :], in_=z[1][:, a:b])
-        nc.vector.tensor_tensor(cells(2, 0, S), h[2, 0], gate_sb[:], MULT)
-        nc.scalar.activation(cells(3, SHARE, S), late[:, HALF : HALF + S - SHARE], COPY)
-        w2_grouped = held.tile([P, N, 4], BF16, name="w2_grouped", tag="late_1", align_bytes=64)
-        nc.vector.tensor_copy(
-            out=w2_grouped[:].rearrange("p (w i) t -> p w t i", i=2),
-            in_=w2_raw[:].rearrange("p t (w i) -> p w t i", i=2),
-        )
+        nc.gpsimd.tensor_tensor(late[3][:], rest[:], gate_sb[:, SHARE:S], MULT)
+        nc.vector.tensor_copy(cells(2, 0, S), late[2][:])
+        nc.scalar.activation(cells(3, SHARE, S), late[3][:], COPY)
+        w2_grouped = held.tile([P, N, 4], BF16, name="w2_grouped", tag="h_rest", align_bytes=64)
+        nc.gpsimd.tensor_scalar(w2_grouped[:], w2_raw[:].rearrange("p t m -> p m t"), 1.0, 0.0, MULT, ADD)
         nc.vector.tensor_copy(out=plane_cells(0, HALF)[:, 2, :], in_=z[2][:, 0:HALF])
+        nc.vector.tensor_copy(out=plane_cells(HALF, 512)[:, 2, :], in_=z[2][:, HALF:512])
         w2q = held.tile([P, N], U32, name="w2q", align_bytes=64)
         w2s = held.tile([P, N], U8, name="w2s", align_bytes=64)
         nc.vector.quantize_mx(
             out=w2q[:].bitcast(FP8X4), scales=w2s[:], in_=w2_grouped[:].rearrange("p m j -> p (m j)")
         )
-        for t, a, b in ((3, 0, HALF), (3, HALF, 512), (2, HALF, 512), (3, 512, 768)):
+        for t, a, b in ((3, 0, HALF), (3, HALF, 512), (3, 512, 768)):
             nc.scalar.copy(out=plane_cells(a, b)[:, t, :], in_=z[t][:, a:b])
         for t, a in ((3, 768), (2, 768)):
             nc.sync.dma_start(out=plane_cells(a, V)[:, t, :], in_=z[t][:, a:V])

from contextlib import ExitStack

import concourse.mybir as mybir

K, T, S, V, H, N = 512, 1024, 512, 1024, 512, 256
FLOPS = 2 * K * H * S + 2 * H * N * V

F32 = mybir.dt.float32
BF16 = mybir.dt.bfloat16
U32 = mybir.dt.uint32
U16 = mybir.dt.uint16
U8 = mybir.dt.uint8
FP8X4 = mybir.dt.float8_e4m3fn_x4
SILU = mybir.ActivationFunctionType.Silu
COPY = mybir.ActivationFunctionType.Copy
MULT = mybir.AluOpType.mult
ADD = mybir.AluOpType.add

P = 128
HALF = 256
SHARE = 128


def tile_picked_voxel_silu_e_kernel(tc, xT, w1, w2, gate, offs, pos1, out):
    nc = tc.nc
    with ExitStack() as ctx:
        held = ctx.enter_context(tc.tile_pool(name="held", bufs=1))
        psum = ctx.enter_context(tc.psum_pool(name="psum", bufs=8))

        x_rows = xT.rearrange("(p j) t -> p j t", j=4)
        w1_rows = w1.rearrange("(p j) c -> p j c", j=4)
        w2_rows = w2.rearrange("(g t i) c -> t g i c", t=4, i=8)

        offs_sb = held.tile([P, S // 16], U16, name="offs_sb")
        pos_sb = held.tile([P, S // 16], U16, name="pos_sb")
        x_raw = []
        for j in range(4):
            t = held.tile([P, T], F32, name=f"x_raw{j}", align_bytes=256)
            nc.sync.dma_start(out=t[:], in_=x_rows[:, j, :])
            x_raw.append(t)
            if j == 0:
                nc.sync.dma_start(offs_sb[:], offs)
        w1_raw = []
        for u in range(2):
            t = held.tile([P, 2, H], F32, name=f"w1_raw{u}", align_bytes=256)
            nc.sync.dma_start(out=t[:], in_=w1_rows[:, 2 * u : 2 * u + 2, :])
            w1_raw.append(t)
        nc.sync.dma_start(pos_sb[:], pos1)
        gate_sb = held.tile([P, S], F32, name="gate_sb", align_bytes=256)
        nc.sync.dma_start(out=gate_sb[:], in_=gate)
        w2_raw = held.tile([P, 4, N], F32, name="w2_raw", align_bytes=256)
        for t in range(4):
            nc.sync.dma_start(out=w2_raw[:, t, :], in_=w2_rows[t])

        warm = held.tile([P, 1], F32, name="warm")
        warm_out = held.tile([P, 1], F32, name="warm_out")
        nc.vector.memset(warm[:], 0.0)
        nc.scalar.activation(warm_out[:], warm[:], SILU)

        z = [held.tile([P, V], F32, name=f"z{t}", align_bytes=256) for t in range(4)]
        for t in range(4):
            nc.vector.memset(z[t][:], 0.0)

        picked = [held.tile([P, HALF, 4], BF16, name=f"picked{e}", align_bytes=64) for e in range(2)]
        for j in range(4):
            nc.vector.tensor_copy(out=picked[0][:, :, j], in_=x_raw[j][:].indirect(offs_sb[:, 0:16]))
            nc.scalar.activation(picked[1][:, :, j], x_raw[j][:].indirect(offs_sb[:, 16:32]), COPY)
        xq = held.tile([P, S], U32, name="xq", align_bytes=64)
        xs = held.tile([P, S], U8, name="xs", align_bytes=64)
        for e in (1, 0):
            nc.vector.quantize_mx(
                out=xq[:, e * HALF : (e + 1) * HALF].bitcast(FP8X4),
                scales=xs[:, e * HALF : (e + 1) * HALF],
                in_=picked[e][:].rearrange("p s j -> p (s j)"),
            )

        w1q = held.tile([P, 4, 128], U32, name="w1q", align_bytes=64)
        w1s = held.tile([P, 4, 128], U8, name="w1s", align_bytes=64)
        grouped = [held.tile([P, 128, 4], BF16, name=f"w1_grouped{t}", align_bytes=64) for t in range(4)]
        for u in range(2):
            w1_from = w1_raw[u][:].rearrange("p e (g t i) -> p t g i e", t=4, i=8)
            for t, copy in ((0, nc.vector.tensor_copy), (3, nc.scalar.copy), (1, nc.vector.tensor_copy), (2, nc.scalar.copy)):
                copy(
                    out=grouped[t][:].rearrange("p (g i) j -> p g i j", i=8)[:, :, :, 2 * u : 2 * u + 2],
                    in_=w1_from[:, t],
                )
        for t in (0, 1, 3, 2):
            nc.vector.quantize_mx(
                out=w1q[:, t, :].bitcast(FP8X4), scales=w1s[:, t, :], in_=grouped[t][:].rearrange("p m j -> p (m j)")
            )

        def first_layer(dst, pieces):
            bank = psum.tile([P, 512], F32, name="bank")
            at = 0
            for t, a, b in pieces:
                nc.tensor.matmul_mx(
                    out=bank[:, at : at + b - a],
                    lhsT=w1q[:, t, :].bitcast(FP8X4),
                    lhsT_scale=w1s[:, t, :],
                    rhs=xq[:, a:b].bitcast(FP8X4),
                    rhs_scale=xs[:, a:b],
                    start=True,
                    stop=True,
                )
                at = at + b - a
            nc.scalar.activation(dst, bank[:, 0:at], SILU)

        def cells(t, a, b):
            return z[t][:].indirect(pos_sb[:, a // 16 : b // 16])

        h = {}
        gated = {t: held.tile([P, HALF], F32, name=f"gated{t}") for t in (0, 1, 3)}

        def silu_of(*pieces):
            tile = held.tile([P, sum(b - a for t, a, b in pieces)], F32, name=f"h{len(h)}", tag=f"h{len(h)}", align_bytes=64)
            first_layer(tile[:], pieces)
            at = 0
            for t, a, b in pieces:
                h[t, a] = tile[:, at : at + b - a]
                at = at + b - a

        def weigh(engine, t, a, b, start):
            engine.tensor_tensor(gated[t][:, a:b], h[t, start][:, a - start : b - start], gate_sb[:, a:b], MULT)

        def scatter_on_vector(t, a, b):
            nc.vector.tensor_copy(cells(t, a, b), gated[t][:, a:b])

        def scatter_on_scalar(t, a, b):
            nc.scalar.activation(cells(t, a, b), gated[t][:, a:b], COPY)

        parts = tuple((a, a + HALF) for a in range(0, V, HALF))
        planes = [held.tile([P, 4 * (b - a)], F32, name=f"planes{a}", align_bytes=256) for a, b in parts]

        def plane_cells(a, b):
            for (start, stop), tile in zip(parts, planes):
                if start <= a < stop:
                    return tile[:].rearrange("p (t v) -> p t v", t=4)[:, :, a - start : b - start]

        silu_of((0, 0, 128))
        silu_of((0, 128, HALF), (1, 0, HALF))
        silu_of((3, 0, SHARE), (0, HALF, S))
        silu_of((1, HALF, S))
        silu_of((2, 0, S))
        nc.vector.tensor_tensor(cells(0, 0, 128), h[0, 0], gate_sb[:, 0:128], MULT)
        weigh(nc.vector, 1, 0, HALF, 0)
        weigh(nc.vector, 0, 128, HALF, 128)
        weigh(nc.vector, 3, 0, SHARE, 0)
        scatter_on_vector(0, 128, HALF)
        late = {}
        for t, a, tag in ((0, HALF, "h1"), (1, HALF, "late1"), (2, 0, "late2")):
            late[t] = held.tile([P, S - a], F32, name=f"late{t}", tag=tag, align_bytes=64)
            nc.gpsimd.tensor_tensor(late[t][:], h[t, a], gate_sb[:, a:S], MULT)
        scatter_on_vector(3, 0, SHARE)
        nc.vector.tensor_copy(cells(0, HALF, S), late[0][:])
        for a, b in parts:
            nc.sync.dma_start(out=plane_cells(a, b)[:, 0, :], in_=z[0][:, a:b])
        scatter_on_scalar(1, 0, HALF)
        late[3] = held.tile([P, S - SHARE], F32, name="late3")
        rest = held.tile([P, S - SHARE], F32, name="h_rest", tag="h_rest", align_bytes=64)
        first_layer(rest[:], ((3, SHARE, HALF), (3, HALF, S)))
        nc.scalar.activation(cells(1, HALF, S), late[1][:], COPY)
        for a, b in parts:
            nc.sync.dma_start(out=plane_cells(a, b)[:, 1, :], in_=z[1][:, a:b])
        nc.gpsimd.tensor_tensor(late[3][:], rest[:], gate_sb[:, SHARE:S], MULT)
        nc.vector.tensor_copy(cells(2, 0, S), late[2][:])
        nc.scalar.activation(cells(3, SHARE, S), late[3][:], COPY)
        w2_grouped = held.tile([P, N, 4], BF16, name="w2_grouped", tag="h_rest", align_bytes=64)
        nc.gpsimd.tensor_scalar(w2_grouped[:], w2_raw[:].rearrange("p t m -> p m t"), 1.0, 0.0, MULT, ADD)
        nc.vector.tensor_copy(out=plane_cells(0, HALF)[:, 2, :], in_=z[2][:, 0:HALF])
        nc.vector.tensor_copy(out=plane_cells(HALF, 512)[:, 2, :], in_=z[2][:, HALF:512])
        w2q = held.tile([P, N], U32, name="w2q", align_bytes=64)
        w2s = held.tile([P, N], U8, name="w2s", align_bytes=64)
        nc.vector.quantize_mx(
            out=w2q[:].bitcast(FP8X4), scales=w2s[:], in_=w2_grouped[:].rearrange("p m j -> p (m j)")
        )
        for t, a, b in ((3, 0, HALF), (3, HALF, 512), (3, 512, 768)):
            nc.scalar.copy(out=plane_cells(a, b)[:, t, :], in_=z[t][:, a:b])
        for t, a in ((3, 768), (2, 768)):
            nc.sync.dma_start(out=plane_cells(a, V)[:, t, :], in_=z[t][:, a:V])

        woven = held.tile([P, 4 * V], BF16, name="woven", align_bytes=64)
        zs = held.tile([P, V], U8, name="zs", align_bytes=64)
        zq = held.tile([P, V], U32, name="zq", align_bytes=64)
        out_rows = out.rearrange("(m p) v -> p m v", p=P)

        def weave_cells(a, b, copy):
            copy(
                out=woven[:, 4 * a : 4 * b].rearrange("p (w i t) -> p w t i", i=2, t=4),
                in_=plane_cells(a, b).rearrange("p t (w i) -> p w t i", i=2),
            )

        def second_layer(dst, m, a, b):
            nc.tensor.matmul_mx(
                out=dst,
                lhsT=w2q[:, m * P : (m + 1) * P].bitcast(FP8X4),
                lhsT_scale=w2s[:, m * P : (m + 1) * P],
                rhs=zq[:, a:b].bitcast(FP8X4),
                rhs_scale=zs[:, a:b],
                start=True,
                stop=True,
            )

        def finish(a, b, copies):
            nc.vector.quantize_mx(out=zq[:, a:b].bitcast(FP8X4), scales=zs[:, a:b], in_=woven[:, 4 * a : 4 * b])
            res = held.tile([P, 2, b - a], F32, name=f"res{a}", align_bytes=256)
            for ms, copy in zip(((0, 1),) if len(copies) == 1 else ((0,), (1,)), copies):
                bank = psum.tile([P, 512], F32, name="bank")
                sums = bank[:, 0 : len(ms) * (b - a)].rearrange("p (m v) -> p m v", m=len(ms))
                for m in ms:
                    second_layer(sums[:, m - ms[0], :], m, a, b)
                copy(out=res[:, ms[0] : ms[-1] + 1, :], in_=sums)
                if b - a == HALF:
                    nc.sync.dma_start(out=out_rows[:, ms[0], a:b], in_=res[:, ms[0], :])
            if b - a == 128:
                nc.sync.dma_start(out=out_rows[:, :, a:b], in_=res[:])

        weave_cells(256, 512, nc.scalar.copy)
        weave_cells(0, 128, nc.vector.tensor_copy)
        nc.vector.tensor_copy(out=plane_cells(512, 768)[:, 2, :], in_=z[2][:, 512:768])
        weave_cells(128, 256, nc.vector.tensor_copy)
        finish(0, 128, [nc.scalar.copy])
        weave_cells(512, 768, nc.vector.tensor_copy)
        finish(128, 256, [nc.scalar.copy])
        finish(256, 512, [nc.scalar.copy] * 2)
        finish(512, 768, [nc.scalar.copy] * 2)
        weave_cells(768, 896, nc.vector.tensor_copy)
        weave_cells(896, V, nc.vector.tensor_copy)
        finish(768, 896, [nc.vector.tensor_copy])
        finish(896, V, [nc.scalar.copy, nc.vector.tensor_copy])
